import numpy as np
import ml_dtypes


def mxq(x, axis, fmt="e4m3"):
    dtype, down = {"e4m3": (ml_dtypes.float8_e4m3fn, 7), "e5m2": (ml_dtypes.float8_e5m2, 14)}[fmt]
    v = np.moveaxis(np.asarray(x, np.float32).astype(ml_dtypes.bfloat16).astype(np.float64), axis, -1)
    blocks = v.reshape(v.shape[:-1] + (-1, 32))
    amax = np.abs(blocks).max(-1, keepdims=True)
    byte = np.maximum(np.where(amax > 0, np.frexp(amax)[1] - 1 + 127, 0) - down, 1)
    scale = np.exp2(byte - 127.0)
    codes = (blocks / scale).astype(np.float32).astype(dtype).astype(np.float64)
    return np.moveaxis((codes * scale).reshape(v.shape), -1, axis)


WIDE = False


def mx_kscale(k):
    if not WIDE:
        return np.ones(k)
    levels = np.array([10, -10, 5, -5, 0])
    if k % 512:
        return np.exp2(np.random.permutation(np.resize(levels, k // 32))).repeat(32)
    a = np.empty((k // 512, 16))
    for p in range(k // 512):
        a[p, :8] = np.random.permutation(np.resize(levels, 8))
        for g in range(8):
            far = levels[np.abs(levels - a[p, g]) >= 10]
            a[p, g + 8] = far[np.random.randint(len(far))]
    return np.exp2(a.ravel()).repeat(32)


def f64(x):
    return np.asarray(x).astype(np.float64)


def striped(idx):
    return np.tile(idx.reshape(-1, 16).T, (8, 1)).astype(np.uint16)


def unstriped(offs):
    return offs[:16].T.reshape(-1).astype(np.int64)


E2M1 = np.array([0.0, 0.5, 1.0, 1.5, 2.0, 3.0, 4.0, 6.0, -0.0, -0.5, -1.0, -1.5, -2.0, -3.0, -4.0, -6.0])


def pack_weight(w, fmt):
    k, n = w.shape
    w = f64(np.asarray(w, np.float32).astype(ml_dtypes.bfloat16)).reshape(k // 32, 32, n)
    amax = np.abs(w).max(1)
    if fmt == "e4m3":
        byte = np.frexp(amax)[1] - 1 + 127 - 7
    else:
        mant, ex = np.frexp(amax / 6.0)
        byte = np.where(mant > 0.5, ex, ex - 1) + 127
    byte = np.clip(np.where(amax > 0, byte, 1), 1, 254)
    scaled = (w * np.exp2(127.0 - byte)[:, None, :]).reshape(k, n).astype(np.float32)
    by_word = np.ascontiguousarray(scaled.reshape(k // 512, 128, 4, n).transpose(0, 1, 3, 2))
    if fmt == "e4m3":
        words = by_word.astype(ml_dtypes.float8_e4m3fn).view(np.uint8)
    else:
        c = by_word.astype(ml_dtypes.float4_e2m1fn).view(np.uint8) & 0xF
        words = (c[..., 0::2] | (c[..., 1::2] << 4)).reshape(k // 512, 128, 2 * n)
    return np.ascontiguousarray(words), np.ascontiguousarray(byte.astype(np.uint8).reshape(k // 512, 16, n))


def unpack_weight(words, scales, fmt):
    g, _, n = scales.shape
    words = np.ascontiguousarray(words).reshape(g, 128, n, -1)
    if fmt == "e4m3":
        vals = words.view(ml_dtypes.float8_e4m3fn).astype(np.float64)
    else:
        nib = np.empty((g, 128, n, 4), np.uint8)
        nib[..., 0::2] = words & 0xF
        nib[..., 1::2] = words >> 4
        vals = E2M1[nib]
    vals = vals * np.repeat(np.exp2(scales.astype(np.float64) - 127.0), 8, axis=1)[..., None]
    return vals.transpose(0, 1, 3, 2).reshape(g * 512, n)


def relu(v):
    return np.maximum(v, 0.0)


K, T, E, C, H, N = 1024, 640, 6, 128, 512, 128
TOP = 4
PAD = 64


def by_expert(wq, xq):
    return np.concatenate([wq[e].T @ xq[:, e * C:(e + 1) * C] for e in range(E)], axis=1)


def setup_inputs():
    n = np.random.standard_normal
    s = mx_kscale(K)[:, None]
    u = mx_kscale(H)
    slot_token = np.empty(E * C, np.int64); pos = np.tile(E * C + np.arange(T) % PAD, (TOP, 1)); taken = np.zeros(T, np.int64)
    liked = np.random.randn(T)
    for e in np.random.permutation(E):
        free = np.flatnonzero(taken < TOP); pick = np.random.permutation(free[np.argsort(-(liked[free] + np.random.gumbel(size=free.size)))[:C]]); slot_token[e * C:(e + 1) * C] = pick
        pos[taken[pick], pick] = e * C + np.arange(C); taken[pick] += 1
    g = np.random.uniform(0.2, 0.8, (TOP, T))
    w1 = [pack_weight(m, "e2m1") for m in n((E, K, H)) / np.sqrt(K) / s[None]]
    w3 = [pack_weight(m, "e2m1") for m in n((E, K, H)) / np.sqrt(K) / s[None] * u[None, None, :]]
    w2 = [pack_weight(m, "e2m1") for m in n((E, H, N)) / np.sqrt(H) / u[None, :, None]]
    x = pack_weight(n((K, T)) * s, "e4m3")
    return {
        "x_words": x[0],
        "x_scales": x[1],
        "w1_words": np.stack([m[0] for m in w1]),
        "w1_scales": np.stack([m[1] for m in w1]),
        "w3_words": np.stack([m[0] for m in w3]),
        "w3_scales": np.stack([m[1] for m in w3]),
        "w2_words": np.stack([m[0] for m in w2]),
        "w2_scales": np.stack([m[1] for m in w2]),
        "gate": np.stack([np.tile(r, (N, 1)) for r in g]).astype(np.float32),
        "offs": striped(slot_token),
        "pos1": striped(pos[0]),
        "pos2": striped(pos[1]),
        "pos3": striped(pos[2]),
        "pos4": striped(pos[3]),
    }


def reference(x_words, x_scales, w1_words, w1_scales, w3_words, w3_scales, w2_words, w2_scales, gate, offs, pos1, pos2, pos3, pos4):
    idx = unstriped(offs)
    w1 = np.stack([unpack_weight(w1_words[e], w1_scales[e], "e2m1") for e in range(E)])
    w3 = np.stack([unpack_weight(w3_words[e], w3_scales[e], "e2m1") for e in range(E)])
    w2 = np.stack([unpack_weight(w2_words[e], w2_scales[e], "e2m1") for e in range(E)])
    xq = unpack_weight(x_words, x_scales, "e4m3")[:, idx]
    h = relu(by_expert(w1, xq))
    h = h * by_expert(w3, xq)
    y = by_expert(w2, mxq(h, 0, "e4m3"))
    y = np.concatenate([y, np.zeros((N, PAD))], axis=1)
    return sum(f64(gate[r]) * y[:, unstriped(p)] for r, p in enumerate((pos1, pos2, pos3, pos4)))

@@ -1,0 +1,230 @@
+from contextlib import ExitStack
+
+import concourse.mybir as mybir
+from concourse.masks import make_identity
+
+K, T, E, C, H, N = 1024, 640, 6, 128, 512, 128
+TOP = 4
+PAD = 64
+S = E * C
+P = 128
+PASSES = K // 512
+FLOPS = 2 * S * (2 * K * H + H * N)
+
+F32 = mybir.dt.float32
+BF16 = mybir.dt.bfloat16
+I32 = mybir.dt.int32
+U32 = mybir.dt.uint32
+U16 = mybir.dt.uint16
+U8 = mybir.dt.uint8
+FP8X4 = mybir.dt.float8_e4m3fn_x4
+FP4X4 = mybir.dt.float4_e2m1fn_x4
+ACT = mybir.ActivationFunctionType
+ALU = mybir.AluOpType
+
+
+def load_scale_rows(queue, plane, rows):
+    groups = rows.shape[0]
+    by_row = rows.rearrange("g (q r) w -> r q g w", r=4)
+    for r in range(4):
+        queue.dma_start(
+            out=plane[r:P:32, :].bitcast(I32).rearrange("q (g w) -> q g w", g=groups),
+            in_=by_row[r].bitcast(I32),
+        )
+
+
+def tile_moe_ecr_glu_relu_kernel(
+    tc, x_words, x_scales, w1_words, w1_scales, w3_words, w3_scales, w2_words, w2_scales,
+    gate, offs, pos1, pos2, pos3, pos4, out,
+):
+    nc = tc.nc
+    with ExitStack() as ctx:
+        keep = ctx.enter_context(tc.tile_pool(name="keep", bufs=1))
+        ring = ctx.enter_context(tc.tile_pool(name="ring", bufs=2))
+        psum = ctx.enter_context(tc.psum_pool(name="psum", bufs=1))
+
+        def bank(b, name):
+            return psum.tile([P, 512], F32, name=name, tag="bank%d" % b)
+
+        xs = keep.tile([P, PASSES * T], U8, name="xs", align_bytes=64)
+        SG = [[0, 1], [2, 3, 4, 5]]
+        w1s = [keep.tile([P, len(g) * PASSES * H], U8, name="w1s%d" % g[0], align_bytes=64) for g in SG]
+        w3s = [keep.tile([P, len(g) * PASSES * H], U8, name="w3s%d" % g[0], align_bytes=64) for g in SG]
+        w2s = keep.tile([P, E * N], U8, name="w2s", align_bytes=64)
+        y = keep.tile([P, S + PAD], F32, name="y", align_bytes=64)
+        wide = ctx.enter_context(tc.tile_pool(name="wide", bufs=6))
+        nc.vector.memset(xs[:].bitcast(I32), 0)
+        nc.vector.memset(w1s[0][:].bitcast(I32), 0)
+        nc.vector.memset(w3s[0][:].bitcast(I32), 0)
+        nc.vector.memset(w2s[:].bitcast(I32), 0)
+        nc.gpsimd.memset(w1s[1][:].bitcast(I32), 0)
+        nc.gpsimd.memset(w3s[1][:].bitcast(I32), 0)
+        offs_t = keep.tile([P, S // 16], U16, name="offs_t")
+        xw = [keep.tile([P, T], I32, name="xw%d" % s, align_bytes=64) for s in range(PASSES)]
+        WG = [[0], [1], [2, 3], [4], [5]]
+        w1w = [keep.tile([P, len(g) * PASSES * 2 * H], U8, name="w1w%d" % g[0], align_bytes=64) for g in WG]
+        w3w = [keep.tile([P, len(g) * PASSES * 2 * H], U8, name="w3w%d" % g[0], align_bytes=64) for g in WG]
+        w2w = keep.tile([P, E * 2 * N], U8, name="w2w", align_bytes=64)
+        pos_t = [keep.tile([P, T // 16], U16, name="pos%d" % r) for r in range(TOP)]
+        pos = (pos1, pos2, pos3, pos4)
+
+        def load_w(queue, tiles, words, gi):
+            g = WG[gi]
+            queue.dma_start(
+                out=tiles[gi][:].bitcast(I32).rearrange("p (g w) -> p g w", g=len(g) * PASSES),
+                in_=words[g[0]:g[-1] + 1].rearrange("e s p b -> p (e s) b").bitcast(I32),
+            )
+
+        def load_x(queue, s):
+            queue.dma_start(out=xw[s][:], in_=x_words[s].rearrange("p t r -> p (t r)").bitcast(I32))
+
+        def load_w2(queue):
+            queue.dma_start(
+                out=w2w[:].bitcast(I32).rearrange("p (e w) -> p e w", e=E),
+                in_=w2_words.rearrange("e s p b -> p (e s) b").bitcast(I32),
+            )
+
+        xs_rows = x_scales
+        w1s_rows = [w1_scales[g[0]:g[-1] + 1].rearrange("e s q w -> (e s) q w") for g in SG]
+        w3s_rows = [w3_scales[g[0]:g[-1] + 1].rearrange("e s q w -> (e s) q w") for g in SG]
+        w2s_rows = w2_scales.rearrange("e s q w -> (e s) q w")
+        gq = keep.tile([P, P], F32, name="gq")
+        q = nc.sync
+        q.dma_start(offs_t[:], offs)
+        load_x(q, 0)
+        load_scale_rows(q, xs, xs_rows)
+        load_x(q, 1)
+        load_w(q, w1w, w1_words, 0)
+        load_scale_rows(q, w1s[0], w1s_rows[0])
+        load_w(q, w3w, w3_words, 0)
+        load_scale_rows(q, w3s[0], w3s_rows[0])
+        load_w(q, w1w, w1_words, 1)
+        load_w(q, w3w, w3_words, 1)
+        load_scale_rows(q, w1s[1], w1s_rows[1])
+        load_w(q, w1w, w1_words, 2)
+        load_scale_rows(q, w3s[1], w3s_rows[1])
+        load_w(q, w3w, w3_words, 2)
+        load_scale_rows(q, w2s, w2s_rows)
+        load_w2(q)
+        load_w(q, w1w, w1_words, 3)
+        load_w(q, w3w, w3_words, 3)
+        load_w(q, w1w, w1_words, 4)
+        load_w(q, w3w, w3_words, 4)
+        q.dma_start(out=gq[:], in_=gate.rearrange("r n t -> (r n t)").rearrange("(q s) -> q s", s=2048)[0:P, 0:P])
+        for r in range(TOP):
+            q.dma_start(pos_t[r][:], pos[r])
+
+        ident = keep.tile([P, P], F32, name="ident")
+        make_identity(nc, ident[:])
+        nc.scalar.activation(y[:, S:S + PAD], ident[:, 0:PAD], ACT.Relu, scale=-1.0)
+        gath = ctx.enter_context(tc.tile_pool(name="gath", bufs=3))
+        xg, xsg = {}, {}
+
+        def gather(g):
+            e = g[0]
+            lst = offs_t[:, e * C // 16:(e + 1) * C // 16]
+            for s in range(PASSES):
+                xg[e, s] = gath.tile([P, C], U32, name="xg%d" % s, align_bytes=64)
+                xsg[e, s] = gath.tile([P, C], U8, name="xsg%d" % s, align_bytes=64)
+                nc.vector.tensor_copy(xg[e, s][:], xw[s][:].bitcast(U32).indirect(lst))
+                nc.vector.tensor_copy(xsg[e, s][:], xs[:, s * T:(s + 1) * T].indirect(lst))
+
+        def first(e, tiles, plane, b, name):
+            gi = [i for i, g in enumerate(WG) if e in g][0]
+            si = [i for i, g in enumerate(SG) if e in g][0]
+            acc = bank(b, name)
+            cols = slice(e * C, (e + 1) * C)
+            for s in range(PASSES):
+                at = ((e - WG[gi][0]) * PASSES + s) * 2 * H
+                nc.tensor.matmul_mx(
+                    out=acc[:],
+                    lhsT=xg[e, s][:].bitcast(FP8X4),
+                    lhsT_scale=xsg[e, s][:],
+                    rhs=tiles[gi][:, at:at + 2 * H].bitcast(FP4X4),
+                    rhs_scale=plane[si][:, ((e - SG[si][0]) * PASSES + s) * H:((e - SG[si][0]) * PASSES + s + 1) * H],
+                    start=(s == 0), stop=(s == PASSES - 1),
+                )
+            return acc[:].rearrange("c (p u v) -> c u p v", u=2, v=2)
+
+        state = {}
+
+        def stage_a(e):
+            a = first(e, w1w, w1s, e % 2, "a")
+            b = first(e, w3w, w3s, 2 + e % 2, "b")
+            ra = ring.tile([P, 2, P, 2], F32, name="ra")
+            nc.scalar.activation(ra[:], a, ACT.Relu)
+            h = ring.tile([P, 2, P, 2], BF16, name="h", align_bytes=64)
+            nc.vector.tensor_tensor(h[:], b, ra[:], ALU.mult)
+            state[e] = h
+
+        def stage_b(e):
+            hw = state[e][:].rearrange("c u p v -> c (u p v)").bitcast(F32)
+            tb = bank(4 + e % 2, "tb")
+            for u in range(2):
+                nc.tensor.transpose(tb[:, u * P:(u + 1) * P], hw[:, u * P:(u + 1) * P], ident[:])
+            ht = ring.tile([P, C, 2], F32, name="ht", align_bytes=64)
+            nc.scalar.copy(ht[:], tb[:, 0:2 * P].rearrange("p (u c) -> p c u", u=2))
+            state[e] = ht
+
+        def stage_c(e):
+            ht = state[e]
+            hq = ring.tile([P, C], U32, name="hq", align_bytes=64)
+            hs = ring.tile([P, C], U8, name="hs", align_bytes=64)
+            nc.vector.quantize_mx(
+                out=hq[:].bitcast(FP8X4), scales=hs[:],
+                in_=ht[:].rearrange("p c u -> p (c u)").bitcast(BF16),
+            )
+            yb = bank(6 + e % 2, "yb")
+            nc.tensor.matmul_mx(
+                out=yb[:, 0:C],
+                lhsT=w2w[:, e * 2 * N:(e + 1) * 2 * N].bitcast(FP4X4),
+                lhsT_scale=w2s[:, e * N:(e + 1) * N],
+                rhs=hq[:].bitcast(FP8X4), rhs_scale=hs[:],
+                start=True, stop=True,
+            )
+            nc.scalar.copy(y[:, e * C:(e + 1) * C], yb[:, 0:C])
+
+        AHEAD = 3
+        for e in range(AHEAD):
+            gather([e])
+        for step in range(E + 2):
+            if step < E:
+                stage_a(step)
+            if 0 <= step - 1 < E:
+                stage_b(step - 1)
+            if 0 <= step - 2 < E:
+                stage_c(step - 2)
+            if step + AHEAD < E:
+                gather([step + AHEAD])
+
+        gb = bank(4, "gb")
+        nc.tensor.transpose(gb[:, 0:P], gq[:], ident[:])
+        gcol = keep.tile([P, TOP, T // P], F32, name="gcol")
+        nc.scalar.copy(gcol[:], gb[:, 0:160].rearrange("t (r j) -> t r j", j=40)[:, :, 0:T // P])
+        CH = T // P
+        acc = [bank(c, "acc") for c in range(CH)]
+        res = keep.tile([P, T], F32, name="res")
+        got = [keep.tile([P, T], F32, name="got%d" % r) for r in range(TOP)]
+        PIECES = [[2, 3], [2, 3], [2, 3], [2, 2, 1]]
+        n_piece = 0
+        for r in range(TOP):
+            c0 = 0
+            for w in PIECES[r]:
+                cols = slice(c0 * P, (c0 + w) * P)
+                nc.vector.tensor_copy(got[r][:, cols], y[:].indirect(pos_t[r][:, cols.start // 16:cols.stop // 16]))
+                fwd = bank(CH + n_piece % 3, "fwd")
+                n_piece = n_piece + 1
+                for j in range(w):
+                    c = c0 + j
+                    nc.tensor.transpose(fwd[:, j * P:(j + 1) * P], got[r][:, c * P:(c + 1) * P], ident[:])
+                for j in range(w):
+                    c = c0 + j
+                    sc = wide.tile([P, P], F32, name="sc")
+                    nc.scalar.activation(sc[:], fwd[:, j * P:(j + 1) * P], ACT.Copy, scale=gcol[:, r, c:c + 1])
+                    nc.tensor.matmul(acc[c][:, 0:P], lhsT=sc[:], rhs=ident[:], is_transpose=True,
+                                     start=(r == 0), stop=(r == TOP - 1))
+                    if r == TOP - 1:
+                        nc.vector.tensor_copy(res[:, c * P:(c + 1) * P], acc[c][:, 0:P])
+                if r == TOP - 1:
+                    nc.sync.dma_start(out=out[:, cols], in_=res[:, cols])
+                c0 = c0 + w

@@ -47,21 +47,23 @@ def tile_moe_ecr_glu_relu_kernel(
             return psum.tile([P, 512], F32, name=name, tag="bank%d" % b)
 
         xs = keep.tile([P, PASSES * T], U8, name="xs", align_bytes=64)
-        SG = [[0, 1], [2, 3, 4, 5]]
+        SG = [[0,1,2,3],[4,5]]
         w1s = [keep.tile([P, len(g) * PASSES * H], U8, name="w1s%d" % g[0], align_bytes=64) for g in SG]
         w3s = [keep.tile([P, len(g) * PASSES * H], U8, name="w3s%d" % g[0], align_bytes=64) for g in SG]
         w2s = keep.tile([P, E * N], U8, name="w2s", align_bytes=64)
         y = keep.tile([P, S + PAD], F32, name="y", align_bytes=64)
         wide = ctx.enter_context(tc.tile_pool(name="wide", bufs=6))
+        ident = keep.tile([P, P], F32, name="ident")
         nc.vector.memset(xs[:].bitcast(I32), 0)
         nc.vector.memset(w1s[0][:].bitcast(I32), 0)
-        nc.vector.memset(w3s[0][:].bitcast(I32), 0)
-        nc.vector.memset(w2s[:].bitcast(I32), 0)
-        nc.gpsimd.memset(w1s[1][:].bitcast(I32), 0)
+        nc.gpsimd.memset(w3s[0][:].bitcast(I32), 0)
+        make_identity(nc, ident[:])
+        nc.gpsimd.memset(w2s[:].bitcast(I32), 0)
+        nc.vector.memset(w1s[1][:].bitcast(I32), 0)
         nc.gpsimd.memset(w3s[1][:].bitcast(I32), 0)
         offs_t = keep.tile([P, S // 16], U16, name="offs_t")
-        xw = [keep.tile([P, T], I32, name="xw%d" % s, align_bytes=64) for s in range(PASSES)]
-        WG = [[0], [1], [2, 3], [4], [5]]
+        xw = keep.tile([P, PASSES * T], I32, name="xw", align_bytes=64)
+        WG = [[0],[1],[2],[3],[4],[5]]
         w1w = [keep.tile([P, len(g) * PASSES * 2 * H], U8, name="w1w%d" % g[0], align_bytes=64) for g in WG]
         w3w = [keep.tile([P, len(g) * PASSES * 2 * H], U8, name="w3w%d" % g[0], align_bytes=64) for g in WG]
         w2w = keep.tile([P, E * 2 * N], U8, name="w2w", align_bytes=64)
@@ -76,7 +78,7 @@ def tile_moe_ecr_glu_relu_kernel(
             )
 
         def load_x(queue, s):
-            queue.dma_start(out=xw[s][:], in_=x_words[s].rearrange("p t r -> p (t r)").bitcast(I32))
+            queue.dma_start(out=xw[:, s * T:(s + 1) * T], in_=x_words[s].rearrange("p t r -> p (t r)").bitcast(I32))
 
         def load_w2(queue):
             queue.dma_start(
@@ -89,125 +91,139 @@ def tile_moe_ecr_glu_relu_kernel(
         w3s_rows = [w3_scales[g[0]:g[-1] + 1].rearrange("e s q w -> (e s) q w") for g in SG]
         w2s_rows = w2_scales.rearrange("e s q w -> (e s) q w")
         gq = keep.tile([P, P], F32, name="gq")
+        gate_last = keep.tile([P, T], F32, name="gate_last")
         q = nc.sync
         q.dma_start(offs_t[:], offs)
         load_x(q, 0)
-        load_scale_rows(q, xs, xs_rows)
         load_x(q, 1)
-        load_w(q, w1w, w1_words, 0)
+        load_scale_rows(q, xs, xs_rows)
         load_scale_rows(q, w1s[0], w1s_rows[0])
-        load_w(q, w3w, w3_words, 0)
+        load_w(q, w1w, w1_words, 0)
         load_scale_rows(q, w3s[0], w3s_rows[0])
+        load_w(q, w3w, w3_words, 0)
         load_w(q, w1w, w1_words, 1)
         load_w(q, w3w, w3_words, 1)
-        load_scale_rows(q, w1s[1], w1s_rows[1])
         load_w(q, w1w, w1_words, 2)
-        load_scale_rows(q, w3s[1], w3s_rows[1])
         load_w(q, w3w, w3_words, 2)
-        load_scale_rows(q, w2s, w2s_rows)
-        load_w2(q)
         load_w(q, w1w, w1_words, 3)
         load_w(q, w3w, w3_words, 3)
+        load_scale_rows(q, w1s[1], w1s_rows[1])
         load_w(q, w1w, w1_words, 4)
+        load_scale_rows(q, w3s[1], w3s_rows[1])
         load_w(q, w3w, w3_words, 4)
+        load_w(q, w1w, w1_words, 5)
+        load_w(q, w3w, w3_words, 5)
+        load_scale_rows(q, w2s, w2s_rows)
+        load_w2(q)
         q.dma_start(out=gq[:], in_=gate.rearrange("r n t -> (r n t)").rearrange("(q s) -> q s", s=2048)[0:P, 0:P])
         for r in range(TOP):
             q.dma_start(pos_t[r][:], pos[r])
+        q.dma_start(out=gate_last[:], in_=gate[TOP - 1])
 
-        ident = keep.tile([P, P], F32, name="ident")
-        make_identity(nc, ident[:])
         nc.scalar.activation(y[:, S:S + PAD], ident[:, 0:PAD], ACT.Relu, scale=-1.0)
-        gath = ctx.enter_context(tc.tile_pool(name="gath", bufs=3))
-        xg, xsg = {}, {}
+        xgw = [keep.tile([P, S], U32, name="xgw%d" % s, align_bytes=64) for s in range(PASSES)]
+        xgs = [keep.tile([P, S], U8, name="xgs%d" % s, align_bytes=64) for s in range(PASSES)]
 
-        def gather(g):
-            e = g[0]
-            lst = offs_t[:, e * C // 16:(e + 1) * C // 16]
+        def gather(dst, window, e0, e1):
             for s in range(PASSES):
-                xg[e, s] = gath.tile([P, C], U32, name="xg%d" % s, align_bytes=64)
-                xsg[e, s] = gath.tile([P, C], U8, name="xsg%d" % s, align_bytes=64)
-                nc.vector.tensor_copy(xg[e, s][:], xw[s][:].bitcast(U32).indirect(lst))
-                nc.vector.tensor_copy(xsg[e, s][:], xs[:, s * T:(s + 1) * T].indirect(lst))
+                nc.vector.tensor_copy(dst[s][:, e0 * C:e1 * C],
+                                      window[:, s * T:(s + 1) * T].indirect(offs_t[:, e0 * C // 16:e1 * C // 16]))
 
-        def first(e, tiles, plane, b, name):
+        xwu = xw[:].bitcast(U32)
+        gather(xgw, xwu, 0, 1)
+        gather(xgs, xs, 0, 2)
+        gather(xgw, xwu, 1, 3)
+        gather(xgs, xs, 2, 4)
+        gather(xgw, xwu, 3, 6)
+        gather(xgs, xs, 4, 6)
+
+        hh, hqs = {}, {}
+        SPLIT = 3 * P
+
+        def operands(e, s, tiles, plane, lo, width):
             gi = [i for i, g in enumerate(WG) if e in g][0]
             si = [i for i, g in enumerate(SG) if e in g][0]
-            acc = bank(b, name)
-            cols = slice(e * C, (e + 1) * C)
-            for s in range(PASSES):
-                at = ((e - WG[gi][0]) * PASSES + s) * 2 * H
-                nc.tensor.matmul_mx(
-                    out=acc[:],
-                    lhsT=xg[e, s][:].bitcast(FP8X4),
-                    lhsT_scale=xsg[e, s][:],
-                    rhs=tiles[gi][:, at:at + 2 * H].bitcast(FP4X4),
-                    rhs_scale=plane[si][:, ((e - SG[si][0]) * PASSES + s) * H:((e - SG[si][0]) * PASSES + s + 1) * H],
-                    start=(s == 0), stop=(s == PASSES - 1),
-                )
-            return acc[:].rearrange("c (p u v) -> c u p v", u=2, v=2)
+            at = ((e - WG[gi][0]) * PASSES + s) * H + lo
+            sat = ((e - SG[si][0]) * PASSES + s) * H + lo
+            return dict(
+                lhsT=xgw[s][:, e * C:(e + 1) * C].bitcast(FP8X4), lhsT_scale=xgs[s][:, e * C:(e + 1) * C],
+                rhs=tiles[gi][:, 2 * at:2 * (at + width)].bitcast(FP4X4),
+                rhs_scale=plane[si][:, sat:sat + width],
+                start=(s == 0), stop=(s == PASSES - 1),
+            )
 
-        state = {}
+        def by_word(ap):
+            return ap.rearrange("c (p u v) -> c u p v", u=2, v=2)
 
-        def stage_a(e):
-            a = first(e, w1w, w1s, e % 2, "a")
-            b = first(e, w3w, w3s, 2 + e % 2, "b")
-            ra = ring.tile([P, 2, P, 2], F32, name="ra")
-            nc.scalar.activation(ra[:], a, ACT.Relu)
-            h = ring.tile([P, 2, P, 2], BF16, name="h", align_bytes=64)
-            nc.vector.tensor_tensor(h[:], b, ra[:], ALU.mult)
-            state[e] = h
-
-        def stage_b(e):
-            hw = state[e][:].rearrange("c u p v -> c (u p v)").bitcast(F32)
-            tb = bank(4 + e % 2, "tb")
+        def turn(e, tb):
+            hw = hh[e][:].rearrange("c u p v -> c (u p v)").bitcast(F32)
             for u in range(2):
-                nc.tensor.transpose(tb[:, u * P:(u + 1) * P], hw[:, u * P:(u + 1) * P], ident[:])
-            ht = ring.tile([P, C, 2], F32, name="ht", align_bytes=64)
-            nc.scalar.copy(ht[:], tb[:, 0:2 * P].rearrange("p (u c) -> p c u", u=2))
-            state[e] = ht
+                nc.tensor.transpose(tb[:, (u + 1) * P:(u + 2) * P], hw[:, u * P:(u + 1) * P], ident[:])
 
-        def stage_c(e):
-            ht = state[e]
-            hq = ring.tile([P, C], U32, name="hq", align_bytes=64)
-            hs = ring.tile([P, C], U8, name="hs", align_bytes=64)
+        def quantise(e, tb):
+            ht = ring.tile([P, C, 2], F32, name="ht", align_bytes=64)
+            nc.scalar.copy(ht[:], tb[:, P:3 * P].rearrange("p (u c) -> p c u", u=2))
+            hq = ring.tile([P, C], U32, name="hq", align_bytes=64, bufs=E)
+            hs = ring.tile([P, C], U8, name="hs", align_bytes=64, bufs=E)
             nc.vector.quantize_mx(
                 out=hq[:].bitcast(FP8X4), scales=hs[:],
                 in_=ht[:].rearrange("p c u -> p (c u)").bitcast(BF16),
             )
-            yb = bank(6 + e % 2, "yb")
-            nc.tensor.matmul_mx(
-                out=yb[:, 0:C],
-                lhsT=w2w[:, e * 2 * N:(e + 1) * 2 * N].bitcast(FP4X4),
-                lhsT_scale=w2s[:, e * N:(e + 1) * N],
-                rhs=hq[:].bitcast(FP8X4), rhs_scale=hs[:],
-                start=True, stop=True,
-            )
-            nc.scalar.copy(y[:, e * C:(e + 1) * C], yb[:, 0:C])
+            hqs[e] = (hq, hs)
 
-        AHEAD = 3
-        for e in range(AHEAD):
-            gather([e])
-        for step in range(E + 2):
-            if step < E:
-                stage_a(step)
-            if 0 <= step - 1 < E:
-                stage_b(step - 1)
-            if 0 <= step - 2 < E:
-                stage_c(step - 2)
-            if step + AHEAD < E:
-                gather([step + AHEAD])
+        def stage_a(e):
+            a = bank(e % 2, "a")
+            for s in range(PASSES):
+                nc.tensor.matmul_mx(out=a[:], **operands(e, s, w1w, w1s, 0, H))
+            ra = ring.tile([P, 2, P, 2], F32, name="ra")
+            nc.scalar.activation(ra[:], by_word(a[:]), ACT.Relu)
+            b0 = bank(2 + e % 2, "b0")
+            b1 = bank(4 + e % 2, "b1")
+            for j in range(4):
+                dst = b0[:, j * P:(j + 1) * P] if j < 3 else b1[:, 0:P]
+                for s in range(PASSES):
+                    nc.tensor.matmul_mx(out=dst, **operands(e, s, w3w, w3s, j * P, P))
+            if e >= 1:
+                turn(e - 1, b1)
+            h = ring.tile([P, 2, P, 2], BF16, name="h", align_bytes=64)
+            nc.vector.tensor_tensor(h[:, :, 0:96, :], by_word(b0[:, 0:SPLIT]), ra[:, :, 0:96, :], ALU.mult)
+            nc.vector.tensor_tensor(h[:, :, 96:P, :], by_word(b1[:, 0:P]), ra[:, :, 96:P, :], ALU.mult)
+            hh[e] = h
+            if e >= 1:
+                quantise(e - 1, b1)
 
-        gb = bank(4, "gb")
+        def second(es, yb):
+            for j, e in enumerate(es):
+                hq, hs = hqs[e]
+                nc.tensor.matmul_mx(
+                    out=yb[:, j * C:(j + 1) * C],
+                    lhsT=w2w[:, e * 2 * N:(e + 1) * 2 * N].bitcast(FP4X4),
+                    lhsT_scale=w2s[:, e * N:(e + 1) * N],
+                    rhs=hq[:].bitcast(FP8X4), rhs_scale=hs[:],
+                    start=True, stop=True,
+                )
+            nc.scalar.copy(y[:, es[0] * C:(es[-1] + 1) * C], yb[:, 0:len(es) * C])
+
+        for step in range(E):
+            stage_a(step)
+        tb = bank(0, "tb")
+        turn(E - 1, tb)
+        quantise(E - 1, tb)
+        second([0, 1, 2, 3], bank(6, "yb"))
+        second([4], bank(7, "yb"))
+        second([5], bank(1, "yb"))
+        gb = bank(2, "gb")
         nc.tensor.transpose(gb[:, 0:P], gq[:], ident[:])
-        gcol = keep.tile([P, TOP, T // P], F32, name="gcol")
-        nc.scalar.copy(gcol[:], gb[:, 0:160].rearrange("t (r j) -> t r j", j=40)[:, :, 0:T // P])
+        gcol = keep.tile([P, TOP - 1, T // P], F32, name="gcol")
+        nc.scalar.copy(gcol[:], gb[:, 0:120].rearrange("t (r j) -> t r j", j=40)[:, :, 0:T // P])
+
         CH = T // P
         acc = [bank(c, "acc") for c in range(CH)]
         res = keep.tile([P, T], F32, name="res")
         got = [keep.tile([P, T], F32, name="got%d" % r) for r in range(TOP)]
-        PIECES = [[2, 3], [2, 3], [2, 3], [2, 2, 1]]
+        PIECES = [[2, 3], [2, 3], [2, 3]]
         n_piece = 0
-        for r in range(TOP):
+        for r in range(TOP - 1):
             c0 = 0
             for w in PIECES[r]:
                 cols = slice(c0 * P, (c0 + w) * P)
@@ -222,9 +238,19 @@ def tile_moe_ecr_glu_relu_kernel(
                     sc = wide.tile([P, P], F32, name="sc")
                     nc.scalar.activation(sc[:], fwd[:, j * P:(j + 1) * P], ACT.Copy, scale=gcol[:, r, c:c + 1])
                     nc.tensor.matmul(acc[c][:, 0:P], lhsT=sc[:], rhs=ident[:], is_transpose=True,
-                                     start=(r == 0), stop=(r == TOP - 1))
-                    if r == TOP - 1:
-                        nc.vector.tensor_copy(res[:, c * P:(c + 1) * P], acc[c][:, 0:P])
-                if r == TOP - 1:
-                    nc.sync.dma_start(out=out[:, cols], in_=res[:, cols])
+                                     start=(r == 0), stop=(r == TOP - 2))
                 c0 = c0 + w
+        r = TOP - 1
+        c0 = 0
+        for w in [2, 2, 1]:
+            cols = slice(c0 * P, (c0 + w) * P)
+            nc.vector.tensor_tensor(got[r][:, cols], y[:].indirect(pos_t[r][:, cols.start // 16:cols.stop // 16]),
+                                    gate_last[:, cols], ALU.mult)
+            c0 = c0 + w
+        c0 = 0
+        for w in [2, 2, 1]:
+            cols = slice(c0 * P, (c0 + w) * P)
+            for c in range(c0, c0 + w):
+                nc.vector.tensor_tensor(res[:, c * P:(c + 1) * P], acc[c][:, 0:P], got[r][:, c * P:(c + 1) * P], ALU.add)
+            nc.sync.dma_start(out=out[:, cols], in_=res[:, cols])
+            c0 = c0 + w

@@ -9,7 +9,16 @@ PAD = 64
 S = E * C
 P = 128
 PASSES = K // 512
+CHUNKS = T // P
+PER_COL = 16
 FLOPS = 2 * S * (2 * K * H + H * N)
+BYTES = PASSES * T * (4 * P + 16) + E * (2 * PASSES * H + N) * (2 * P + 16) + 4 * TOP * T + 2 * P * (S + TOP * T) // PER_COL + 4 * N * T
+
+SCALE_RUNS = ((0, 4), (4, 6))
+TURNED_PIECES = ((0, 2), (2, 5))
+FUSED_PIECES = ((0, 2), (2, 4), (4, 5))
+GATE_ROW = 2048
+GATE_ROWS_PER_LIST = N * T // GATE_ROW
 
 F32 = mybir.dt.float32
 BF16 = mybir.dt.bfloat16
@@ -23,14 +32,28 @@ ACT = mybir.ActivationFunctionType
 ALU = mybir.AluOpType
 
 
-def load_scale_rows(queue, plane, rows):
-    groups = rows.shape[0]
+def load_plane(nc, plane, rows):
     by_row = rows.rearrange("g (q r) w -> r q g w", r=4)
     for r in range(4):
-        queue.dma_start(
-            out=plane[r:P:32, :].bitcast(I32).rearrange("q (g w) -> q g w", g=groups),
+        nc.sync.dma_start(
+            out=plane[r:P:32, :].bitcast(I32).rearrange("q (g w) -> q g w", g=rows.shape[0]),
             in_=by_row[r].bitcast(I32),
         )
+
+
+def load_words(nc, tile, words):
+    nc.sync.dma_start(
+        out=tile[:].bitcast(I32).rearrange("p (g w) -> p g w", g=words.shape[0]),
+        in_=words.rearrange("g p b -> p g b").bitcast(I32),
+    )
+
+
+def entries(list_tile, first, last):
+    return list_tile[:, first // PER_COL:last // PER_COL]
+
+
+def by_pair(ap):
+    return ap.rearrange("c (p u v) -> c u p v", u=2, v=2)
 
 
 def tile_moe_ecr_glu_relu_kernel(
@@ -43,214 +66,189 @@ def tile_moe_ecr_glu_relu_kernel(
         ring = ctx.enter_context(tc.tile_pool(name="ring", bufs=2))
         psum = ctx.enter_context(tc.psum_pool(name="psum", bufs=1))
 
-        def bank(b, name):
-            return psum.tile([P, 512], F32, name=name, tag="bank%d" % b)
+        def bank(b):
+            return psum.tile([P, 512], F32, name="bank", tag="bank%d" % b)
 
-        xs = keep.tile([P, PASSES * T], U8, name="xs", align_bytes=64)
-        SG = [[0,1,2,3],[4,5]]
-        w1s = [keep.tile([P, len(g) * PASSES * H], U8, name="w1s%d" % g[0], align_bytes=64) for g in SG]
-        w3s = [keep.tile([P, len(g) * PASSES * H], U8, name="w3s%d" % g[0], align_bytes=64) for g in SG]
-        w2s = keep.tile([P, E * N], U8, name="w2s", align_bytes=64)
+        x_plane = keep.tile([P, PASSES * T], U8, name="x_plane", align_bytes=64)
+        w1_planes = [keep.tile([P, (e1 - e0) * PASSES * H], U8, name="w1_plane%d" % e0, align_bytes=64)
+                     for e0, e1 in SCALE_RUNS]
+        w3_planes = [keep.tile([P, (e1 - e0) * PASSES * H], U8, name="w3_plane%d" % e0, align_bytes=64)
+                     for e0, e1 in SCALE_RUNS]
+        w2_plane = keep.tile([P, E * N], U8, name="w2_plane", align_bytes=64)
         y = keep.tile([P, S + PAD], F32, name="y", align_bytes=64)
-        wide = ctx.enter_context(tc.tile_pool(name="wide", bufs=6))
+        scaled_pool = ctx.enter_context(tc.tile_pool(name="scaled", bufs=6))
         ident = keep.tile([P, P], F32, name="ident")
-        nc.vector.memset(xs[:].bitcast(I32), 0)
-        nc.vector.memset(w1s[0][:].bitcast(I32), 0)
-        nc.gpsimd.memset(w3s[0][:].bitcast(I32), 0)
+        nc.vector.memset(x_plane[:].bitcast(I32), 0)
+        nc.vector.memset(w1_planes[0][:].bitcast(I32), 0)
+        nc.gpsimd.memset(w3_planes[0][:].bitcast(I32), 0)
         make_identity(nc, ident[:])
-        nc.gpsimd.memset(w2s[:].bitcast(I32), 0)
-        nc.vector.memset(w1s[1][:].bitcast(I32), 0)
-        nc.gpsimd.memset(w3s[1][:].bitcast(I32), 0)
-        offs_t = keep.tile([P, S // 16], U16, name="offs_t")
-        xw = keep.tile([P, PASSES * T], I32, name="xw", align_bytes=64)
-        WG = [[0],[1],[2],[3],[4],[5]]
-        w1w = [keep.tile([P, len(g) * PASSES * 2 * H], U8, name="w1w%d" % g[0], align_bytes=64) for g in WG]
-        w3w = [keep.tile([P, len(g) * PASSES * 2 * H], U8, name="w3w%d" % g[0], align_bytes=64) for g in WG]
-        w2w = keep.tile([P, E * 2 * N], U8, name="w2w", align_bytes=64)
-        pos_t = [keep.tile([P, T // 16], U16, name="pos%d" % r) for r in range(TOP)]
-        pos = (pos1, pos2, pos3, pos4)
+        nc.gpsimd.memset(w2_plane[:].bitcast(I32), 0)
+        nc.vector.memset(w1_planes[1][:].bitcast(I32), 0)
+        nc.gpsimd.memset(w3_planes[1][:].bitcast(I32), 0)
 
-        def load_w(queue, tiles, words, gi):
-            g = WG[gi]
-            queue.dma_start(
-                out=tiles[gi][:].bitcast(I32).rearrange("p (g w) -> p g w", g=len(g) * PASSES),
-                in_=words[g[0]:g[-1] + 1].rearrange("e s p b -> p (e s) b").bitcast(I32),
-            )
-
-        def load_x(queue, s):
-            queue.dma_start(out=xw[:, s * T:(s + 1) * T], in_=x_words[s].rearrange("p t r -> p (t r)").bitcast(I32))
-
-        def load_w2(queue):
-            queue.dma_start(
-                out=w2w[:].bitcast(I32).rearrange("p (e w) -> p e w", e=E),
-                in_=w2_words.rearrange("e s p b -> p (e s) b").bitcast(I32),
-            )
-
-        xs_rows = x_scales
-        w1s_rows = [w1_scales[g[0]:g[-1] + 1].rearrange("e s q w -> (e s) q w") for g in SG]
-        w3s_rows = [w3_scales[g[0]:g[-1] + 1].rearrange("e s q w -> (e s) q w") for g in SG]
-        w2s_rows = w2_scales.rearrange("e s q w -> (e s) q w")
-        gq = keep.tile([P, P], F32, name="gq")
+        offs_t = keep.tile([P, S // PER_COL], U16, name="offs_t")
+        x_t = keep.tile([P, PASSES * T], I32, name="x_t", align_bytes=64)
+        w1_t = [keep.tile([P, PASSES * 2 * H], U8, name="w1_t%d" % e, align_bytes=64) for e in range(E)]
+        w3_t = [keep.tile([P, PASSES * 2 * H], U8, name="w3_t%d" % e, align_bytes=64) for e in range(E)]
+        w2_t = keep.tile([P, E * 2 * N], U8, name="w2_t", align_bytes=64)
+        pos_t = [keep.tile([P, T // PER_COL], U16, name="pos_t%d" % r) for r in range(TOP)]
+        gate_rows = keep.tile([P, P], F32, name="gate_rows")
         gate_last = keep.tile([P, T], F32, name="gate_last")
-        q = nc.sync
-        q.dma_start(offs_t[:], offs)
-        load_x(q, 0)
-        load_x(q, 1)
-        load_scale_rows(q, xs, xs_rows)
-        load_scale_rows(q, w1s[0], w1s_rows[0])
-        load_w(q, w1w, w1_words, 0)
-        load_scale_rows(q, w3s[0], w3s_rows[0])
-        load_w(q, w3w, w3_words, 0)
-        load_w(q, w1w, w1_words, 1)
-        load_w(q, w3w, w3_words, 1)
-        load_w(q, w1w, w1_words, 2)
-        load_w(q, w3w, w3_words, 2)
-        load_w(q, w1w, w1_words, 3)
-        load_w(q, w3w, w3_words, 3)
-        load_scale_rows(q, w1s[1], w1s_rows[1])
-        load_w(q, w1w, w1_words, 4)
-        load_scale_rows(q, w3s[1], w3s_rows[1])
-        load_w(q, w3w, w3_words, 4)
-        load_w(q, w1w, w1_words, 5)
-        load_w(q, w3w, w3_words, 5)
-        load_scale_rows(q, w2s, w2s_rows)
-        load_w2(q)
-        q.dma_start(out=gq[:], in_=gate.rearrange("r n t -> (r n t)").rearrange("(q s) -> q s", s=2048)[0:P, 0:P])
-        for r in range(TOP):
-            q.dma_start(pos_t[r][:], pos[r])
-        q.dma_start(out=gate_last[:], in_=gate[TOP - 1])
+
+        nc.sync.dma_start(offs_t[:], offs)
+        for s in range(PASSES):
+            nc.sync.dma_start(out=x_t[:, s * T:(s + 1) * T],
+                              in_=x_words[s].rearrange("p t r -> p (t r)").bitcast(I32))
+        load_plane(nc, x_plane, x_scales)
+        for run, (e0, e1) in enumerate(SCALE_RUNS):
+            for e in range(e0, e1):
+                for w_t, words, w_planes, scales in ((w1_t, w1_words, w1_planes, w1_scales),
+                                                     (w3_t, w3_words, w3_planes, w3_scales)):
+                    if e == e0:
+                        load_plane(nc, w_planes[run], scales[e0:e1].rearrange("e s q w -> (e s) q w"))
+                    load_words(nc, w_t[e], words[e])
+        load_plane(nc, w2_plane, w2_scales.rearrange("e s q w -> (e s) q w"))
+        load_words(nc, w2_t, w2_words.rearrange("e s p b -> (e s) p b"))
+        nc.sync.dma_start(
+            out=gate_rows[:],
+            in_=gate.rearrange("r n t -> (r n t)").rearrange("(q w) -> q w", w=GATE_ROW)[0:P, 0:P],
+        )
+        for r, pos in enumerate((pos1, pos2, pos3, pos4)):
+            nc.sync.dma_start(pos_t[r][:], pos)
+        nc.sync.dma_start(out=gate_last[:], in_=gate[TOP - 1])
 
         nc.scalar.activation(y[:, S:S + PAD], ident[:, 0:PAD], ACT.Relu, scale=-1.0)
-        xgw = [keep.tile([P, S], U32, name="xgw%d" % s, align_bytes=64) for s in range(PASSES)]
-        xgs = [keep.tile([P, S], U8, name="xgs%d" % s, align_bytes=64) for s in range(PASSES)]
 
-        def gather(dst, window, e0, e1):
+        tokens = {}
+
+        def gather_tokens(e0, e1, room):
+            offsets = entries(offs_t, e0 * C, e1 * C)
+            words = [keep.tile([P, (e1 - e0) * C], U32, name="words", tag="words%d%d" % (room, s), align_bytes=64)
+                     for s in range(PASSES)]
+            planes = [keep.tile([P, (e1 - e0) * C], U8, name="planes", tag="planes%d%d" % (room, s), align_bytes=64)
+                      for s in range(PASSES)]
             for s in range(PASSES):
-                nc.vector.tensor_copy(dst[s][:, e0 * C:e1 * C],
-                                      window[:, s * T:(s + 1) * T].indirect(offs_t[:, e0 * C // 16:e1 * C // 16]))
-
-        xwu = xw[:].bitcast(U32)
-        gather(xgw, xwu, 0, 1)
-        gather(xgs, xs, 0, 2)
-        gather(xgw, xwu, 1, 3)
-        gather(xgs, xs, 2, 4)
-        gather(xgw, xwu, 3, 6)
-        gather(xgs, xs, 4, 6)
-
-        hh, hqs = {}, {}
-        SPLIT = 3 * P
-
-        def operands(e, s, tiles, plane, lo, width):
-            gi = [i for i, g in enumerate(WG) if e in g][0]
-            si = [i for i, g in enumerate(SG) if e in g][0]
-            at = ((e - WG[gi][0]) * PASSES + s) * H + lo
-            sat = ((e - SG[si][0]) * PASSES + s) * H + lo
-            return dict(
-                lhsT=xgw[s][:, e * C:(e + 1) * C].bitcast(FP8X4), lhsT_scale=xgs[s][:, e * C:(e + 1) * C],
-                rhs=tiles[gi][:, 2 * at:2 * (at + width)].bitcast(FP4X4),
-                rhs_scale=plane[si][:, sat:sat + width],
-                start=(s == 0), stop=(s == PASSES - 1),
-            )
-
-        def by_word(ap):
-            return ap.rearrange("c (p u v) -> c u p v", u=2, v=2)
-
-        def turn(e, tb):
-            hw = hh[e][:].rearrange("c u p v -> c (u p v)").bitcast(F32)
-            for u in range(2):
-                nc.tensor.transpose(tb[:, (u + 1) * P:(u + 2) * P], hw[:, u * P:(u + 1) * P], ident[:])
-
-        def quantise(e, tb):
-            ht = ring.tile([P, C, 2], F32, name="ht", align_bytes=64)
-            nc.scalar.copy(ht[:], tb[:, P:3 * P].rearrange("p (u c) -> p c u", u=2))
-            hq = ring.tile([P, C], U32, name="hq", align_bytes=64, bufs=E)
-            hs = ring.tile([P, C], U8, name="hs", align_bytes=64, bufs=E)
-            nc.vector.quantize_mx(
-                out=hq[:].bitcast(FP8X4), scales=hs[:],
-                in_=ht[:].rearrange("p c u -> p (c u)").bitcast(BF16),
-            )
-            hqs[e] = (hq, hs)
-
-        def stage_a(e):
-            a = bank(e % 2, "a")
+                nc.vector.tensor_copy(words[s][:], x_t[:].bitcast(U32)[:, s * T:(s + 1) * T].indirect(offsets))
             for s in range(PASSES):
-                nc.tensor.matmul_mx(out=a[:], **operands(e, s, w1w, w1s, 0, H))
-            ra = ring.tile([P, 2, P, 2], F32, name="ra")
-            nc.scalar.activation(ra[:], by_word(a[:]), ACT.Relu)
-            b0 = bank(2 + e % 2, "b0")
-            b1 = bank(4 + e % 2, "b1")
-            for j in range(4):
-                dst = b0[:, j * P:(j + 1) * P] if j < 3 else b1[:, 0:P]
+                nc.vector.tensor_copy(planes[s][:], x_plane[:, s * T:(s + 1) * T].indirect(offsets))
+            for e in range(e0, e1):
                 for s in range(PASSES):
-                    nc.tensor.matmul_mx(out=dst, **operands(e, s, w3w, w3s, j * P, P))
-            if e >= 1:
-                turn(e - 1, b1)
-            h = ring.tile([P, 2, P, 2], BF16, name="h", align_bytes=64)
-            nc.vector.tensor_tensor(h[:, :, 0:96, :], by_word(b0[:, 0:SPLIT]), ra[:, :, 0:96, :], ALU.mult)
-            nc.vector.tensor_tensor(h[:, :, 96:P, :], by_word(b1[:, 0:P]), ra[:, :, 96:P, :], ALU.mult)
-            hh[e] = h
-            if e >= 1:
-                quantise(e - 1, b1)
+                    cols = slice((e - e0) * C, (e - e0 + 1) * C)
+                    tokens[e, s] = (words[s][:, cols], planes[s][:, cols])
 
-        def second(es, yb):
-            for j, e in enumerate(es):
-                hq, hs = hqs[e]
+        def first_layer(dst, e, w_t, w_planes, i0, width):
+            run = [j for j, (e0, e1) in enumerate(SCALE_RUNS) if e0 <= e < e1][0]
+            for s in range(PASSES):
+                word0 = s * H + i0
+                byte0 = ((e - SCALE_RUNS[run][0]) * PASSES + s) * H + i0
                 nc.tensor.matmul_mx(
-                    out=yb[:, j * C:(j + 1) * C],
-                    lhsT=w2w[:, e * 2 * N:(e + 1) * 2 * N].bitcast(FP4X4),
-                    lhsT_scale=w2s[:, e * N:(e + 1) * N],
-                    rhs=hq[:].bitcast(FP8X4), rhs_scale=hs[:],
+                    out=dst,
+                    lhsT=tokens[e, s][0].bitcast(FP8X4), lhsT_scale=tokens[e, s][1],
+                    rhs=w_t[e][:, 2 * word0:2 * (word0 + width)].bitcast(FP4X4),
+                    rhs_scale=w_planes[run][:, byte0:byte0 + width],
+                    start=(s == 0), stop=(s == PASSES - 1),
+                )
+
+        hidden, quantised = {}, {}
+
+        def turn(e, dst):
+            pairs = hidden[e][:].rearrange("c u p v -> c (u p v)").bitcast(F32)
+            for u in range(2):
+                nc.tensor.transpose(dst[:, u * P:(u + 1) * P], pairs[:, u * P:(u + 1) * P], ident[:])
+
+        def quantise(e, src):
+            turned = ring.tile([P, C, 2], F32, name="turned", align_bytes=64)
+            nc.scalar.copy(turned[:], src.rearrange("p (u c) -> p c u", u=2))
+            h_words = ring.tile([P, C], U32, name="h_words", align_bytes=64, bufs=E)
+            h_plane = ring.tile([P, C], U8, name="h_plane", align_bytes=64, bufs=E)
+            nc.vector.quantize_mx(
+                out=h_words[:].bitcast(FP8X4), scales=h_plane[:],
+                in_=turned[:].rearrange("p c u -> p (c u)").bitcast(BF16),
+            )
+            quantised[e] = (h_words, h_plane)
+
+        def expert(e, to_turn):
+            a = bank(e % 2)
+            first_layer(a[:], e, w1_t, w1_planes, 0, H)
+            relu_a = ring.tile([P, 2, P, 2], F32, name="relu_a")
+            nc.scalar.activation(relu_a[:], by_pair(a[:]), ACT.Relu)
+            h = ring.tile([P, 2, P, 2], BF16, name="h", align_bytes=64, bufs=3)
+            hidden[e] = h
+            if not to_turn:
+                b = bank(2 + e % 2)
+                first_layer(b[:], e, w3_t, w3_planes, 0, H)
+                nc.vector.tensor_tensor(h[:], by_pair(b[:]), relu_a[:], ALU.mult)
+                return
+            halves = [bank(2 + e % 2), bank(4 + e % 2)]
+            for j in range(4):
+                first_layer(halves[j // 2][:, (j % 2) * P:(j % 2 + 1) * P], e, w3_t, w3_planes, j * P, P)
+            free = [half[:, 2 * P:4 * P] for half in halves[2 - len(to_turn):]]
+            for earlier, room in zip(to_turn, free):
+                turn(earlier, room)
+            for j, half in enumerate(halves):
+                ps = slice(j * P // 2, (j + 1) * P // 2)
+                nc.vector.tensor_tensor(h[:, :, ps, :], by_pair(half[:, 0:2 * P]), relu_a[:, :, ps, :], ALU.mult)
+            for earlier, room in zip(to_turn, free):
+                quantise(earlier, room)
+
+        def second_layer(e0, e1, dst):
+            for e in range(e0, e1):
+                nc.tensor.matmul_mx(
+                    out=dst[:, (e - e0) * C:(e - e0 + 1) * C],
+                    lhsT=w2_t[:, e * 2 * N:(e + 1) * 2 * N].bitcast(FP4X4),
+                    lhsT_scale=w2_plane[:, e * N:(e + 1) * N],
+                    rhs=quantised[e][0][:].bitcast(FP8X4), rhs_scale=quantised[e][1][:],
                     start=True, stop=True,
                 )
-            nc.scalar.copy(y[:, es[0] * C:(es[-1] + 1) * C], yb[:, 0:len(es) * C])
+            nc.scalar.copy(y[:, e0 * C:e1 * C], dst[:, 0:(e1 - e0) * C])
 
-        for step in range(E):
-            stage_a(step)
-        tb = bank(0, "tb")
-        turn(E - 1, tb)
-        quantise(E - 1, tb)
-        second([0, 1, 2, 3], bank(6, "yb"))
-        second([4], bank(7, "yb"))
-        second([5], bank(1, "yb"))
-        gb = bank(2, "gb")
-        nc.tensor.transpose(gb[:, 0:P], gq[:], ident[:])
-        gcol = keep.tile([P, TOP - 1, T // P], F32, name="gcol")
-        nc.scalar.copy(gcol[:], gb[:, 0:120].rearrange("t (r j) -> t r j", j=40)[:, :, 0:T // P])
+        gather_tokens(0, 1, 0)
+        gather_tokens(1, 3, 1)
+        gather_tokens(3, 4, 2)
+        TURNS = ((), (), (0, 1), (), (2,), (3, 4))
+        for e in range(E):
+            expert(e, TURNS[e])
+            if e == 0:
+                gather_tokens(4, 5, 0)
+            if e == 2:
+                gather_tokens(5, 6, 1)
+        last_turn = bank(0)[:, 0:2 * P]
+        turn(E - 1, last_turn)
+        quantise(E - 1, last_turn)
+        second_layer(0, 3, bank(6))
+        second_layer(3, 5, bank(7))
+        second_layer(5, 6, bank(1))
 
-        CH = T // P
-        acc = [bank(c, "acc") for c in range(CH)]
-        res = keep.tile([P, T], F32, name="res")
-        got = [keep.tile([P, T], F32, name="got%d" % r) for r in range(TOP)]
-        PIECES = [[2, 3], [2, 3], [2, 3]]
-        n_piece = 0
+        gate_bank = bank(2)
+        nc.tensor.transpose(gate_bank[:, 0:P], gate_rows[:], ident[:])
+        gate_col = keep.tile([P, TOP - 1, CHUNKS], F32, name="gate_col")
+        nc.scalar.copy(
+            gate_col[:],
+            gate_bank[:, 0:(TOP - 1) * GATE_ROWS_PER_LIST].rearrange("t (r j) -> t r j", r=TOP - 1)[:, :, 0:CHUNKS],
+        )
+
+        sums = [bank(c) for c in range(CHUNKS)]
+        result = keep.tile([P, T], F32, name="result")
+        fetched = [keep.tile([P, T], F32, name="fetched%d" % r) for r in range(TOP)]
         for r in range(TOP - 1):
-            c0 = 0
-            for w in PIECES[r]:
-                cols = slice(c0 * P, (c0 + w) * P)
-                nc.vector.tensor_copy(got[r][:, cols], y[:].indirect(pos_t[r][:, cols.start // 16:cols.stop // 16]))
-                fwd = bank(CH + n_piece % 3, "fwd")
-                n_piece = n_piece + 1
-                for j in range(w):
-                    c = c0 + j
-                    nc.tensor.transpose(fwd[:, j * P:(j + 1) * P], got[r][:, c * P:(c + 1) * P], ident[:])
-                for j in range(w):
-                    c = c0 + j
-                    sc = wide.tile([P, P], F32, name="sc")
-                    nc.scalar.activation(sc[:], fwd[:, j * P:(j + 1) * P], ACT.Copy, scale=gcol[:, r, c:c + 1])
-                    nc.tensor.matmul(acc[c][:, 0:P], lhsT=sc[:], rhs=ident[:], is_transpose=True,
+            for j, (c0, c1) in enumerate(TURNED_PIECES):
+                nc.vector.tensor_copy(fetched[r][:, c0 * P:c1 * P], y[:].indirect(entries(pos_t[r], c0 * P, c1 * P)))
+                by_token = bank(CHUNKS + (r * len(TURNED_PIECES) + j) % 3)
+                for c in range(c0, c1):
+                    nc.tensor.transpose(by_token[:, (c - c0) * P:(c - c0 + 1) * P],
+                                        fetched[r][:, c * P:(c + 1) * P], ident[:])
+                for c in range(c0, c1):
+                    scaled = scaled_pool.tile([P, P], F32, name="scaled")
+                    nc.scalar.activation(scaled[:], by_token[:, (c - c0) * P:(c - c0 + 1) * P], ACT.Copy,
+                                         scale=gate_col[:, r, c:c + 1])
+                    nc.tensor.matmul(sums[c][:, 0:P], lhsT=scaled[:], rhs=ident[:], is_transpose=True,
                                      start=(r == 0), stop=(r == TOP - 2))
-                c0 = c0 + w
-        r = TOP - 1
-        c0 = 0
-        for w in [2, 2, 1]:
-            cols = slice(c0 * P, (c0 + w) * P)
-            nc.vector.tensor_tensor(got[r][:, cols], y[:].indirect(pos_t[r][:, cols.start // 16:cols.stop // 16]),
-                                    gate_last[:, cols], ALU.mult)
-            c0 = c0 + w
-        c0 = 0
-        for w in [2, 2, 1]:
-            cols = slice(c0 * P, (c0 + w) * P)
-            for c in range(c0, c0 + w):
-                nc.vector.tensor_tensor(res[:, c * P:(c + 1) * P], acc[c][:, 0:P], got[r][:, c * P:(c + 1) * P], ALU.add)
-            nc.sync.dma_start(out=out[:, cols], in_=res[:, cols])
-            c0 = c0 + w
+        last = fetched[TOP - 1]
+        for c0, c1 in FUSED_PIECES:
+            nc.vector.tensor_tensor(last[:, c0 * P:c1 * P], y[:].indirect(entries(pos_t[TOP - 1], c0 * P, c1 * P)),
+                                    gate_last[:, c0 * P:c1 * P], ALU.mult)
+        for c0, c1 in FUSED_PIECES:
+            for c in range(c0, c1):
+                nc.vector.tensor_tensor(result[:, c * P:(c + 1) * P], sums[c][:, 0:P], last[:, c * P:(c + 1) * P],
+                                        ALU.add)
+            nc.sync.dma_start(out=out[:, c0 * P:c1 * P], in_=result[:, c0 * P:c1 * P])

@@ -9,16 +9,12 @@ PAD = 64
 S = E * C
 P = 128
 PASSES = K // 512
-CHUNKS = T // P
 PER_COL = 16
 FLOPS = 2 * S * (2 * K * H + H * N)
 BYTES = PASSES * T * (4 * P + 16) + E * (2 * PASSES * H + N) * (2 * P + 16) + 4 * TOP * T + 2 * P * (S + TOP * T) // PER_COL + 4 * N * T
 
 SCALE_RUNS = ((0, 4), (4, 6))
-TURNED_PIECES = ((0, 2), (2, 5))
-FUSED_PIECES = ((0, 2), (2, 4), (4, 5))
-GATE_ROW = 2048
-GATE_ROWS_PER_LIST = N * T // GATE_ROW
+STORE_PIECES = ((0, 384), (384, T))
 
 F32 = mybir.dt.float32
 BF16 = mybir.dt.bfloat16
@@ -76,7 +72,6 @@ def tile_moe_ecr_glu_relu_kernel(
                      for e0, e1 in SCALE_RUNS]
         w2_plane = keep.tile([P, E * N], U8, name="w2_plane", align_bytes=64)
         y = keep.tile([P, S + PAD], F32, name="y", align_bytes=64)
-        scaled_pool = ctx.enter_context(tc.tile_pool(name="scaled", bufs=6))
         ident = keep.tile([P, P], F32, name="ident")
         nc.vector.memset(x_plane[:].bitcast(I32), 0)
         nc.vector.memset(w1_planes[0][:].bitcast(I32), 0)
@@ -92,8 +87,7 @@ def tile_moe_ecr_glu_relu_kernel(
         w3_t = [keep.tile([P, PASSES * 2 * H], U8, name="w3_t%d" % e, align_bytes=64) for e in range(E)]
         w2_t = keep.tile([P, E * 2 * N], U8, name="w2_t", align_bytes=64)
         pos_t = [keep.tile([P, T // PER_COL], U16, name="pos_t%d" % r) for r in range(TOP)]
-        gate_rows = keep.tile([P, P], F32, name="gate_rows")
-        gate_last = keep.tile([P, T], F32, name="gate_last")
+        gate_t = [keep.tile([P, T], F32, name="gate_t%d" % r) for r in range(TOP)]
 
         nc.sync.dma_start(offs_t[:], offs)
         for s in range(PASSES):
@@ -109,13 +103,10 @@ def tile_moe_ecr_glu_relu_kernel(
                     load_words(nc, w_t[e], words[e])
         load_plane(nc, w2_plane, w2_scales.rearrange("e s q w -> (e s) q w"))
         load_words(nc, w2_t, w2_words.rearrange("e s p b -> (e s) p b"))
-        nc.sync.dma_start(
-            out=gate_rows[:],
-            in_=gate.rearrange("r n t -> (r n t)").rearrange("(q w) -> q w", w=GATE_ROW)[0:P, 0:P],
-        )
         for r, pos in enumerate((pos1, pos2, pos3, pos4)):
             nc.sync.dma_start(pos_t[r][:], pos)
-        nc.sync.dma_start(out=gate_last[:], in_=gate[TOP - 1])
+        for r in range(TOP):
+            nc.sync.dma_start(out=gate_t[r][:], in_=gate[r])
 
         nc.scalar.activation(y[:, S:S + PAD], ident[:, 0:PAD], ACT.Relu, scale=-1.0)
 
@@ -219,36 +210,13 @@ def tile_moe_ecr_glu_relu_kernel(
         second_layer(3, 5, bank(7))
         second_layer(5, 6, bank(1))
 
-        gate_bank = bank(2)
-        nc.tensor.transpose(gate_bank[:, 0:P], gate_rows[:], ident[:])
-        gate_col = keep.tile([P, TOP - 1, CHUNKS], F32, name="gate_col")
-        nc.scalar.copy(
-            gate_col[:],
-            gate_bank[:, 0:(TOP - 1) * GATE_ROWS_PER_LIST].rearrange("t (r j) -> t r j", r=TOP - 1)[:, :, 0:CHUNKS],
-        )
-
-        sums = [bank(c) for c in range(CHUNKS)]
+        product = [keep.tile([P, T], F32, name="product%d" % r) for r in range(TOP)]
+        pair = [keep.tile([P, T], F32, name="pair%d" % j) for j in range(TOP // 2)]
         result = keep.tile([P, T], F32, name="result")
-        fetched = [keep.tile([P, T], F32, name="fetched%d" % r) for r in range(TOP)]
-        for r in range(TOP - 1):
-            for j, (c0, c1) in enumerate(TURNED_PIECES):
-                nc.vector.tensor_copy(fetched[r][:, c0 * P:c1 * P], y[:].indirect(entries(pos_t[r], c0 * P, c1 * P)))
-                by_token = bank(CHUNKS + (r * len(TURNED_PIECES) + j) % 3)
-                for c in range(c0, c1):
-                    nc.tensor.transpose(by_token[:, (c - c0) * P:(c - c0 + 1) * P],
-                                        fetched[r][:, c * P:(c + 1) * P], ident[:])
-                for c in range(c0, c1):
-                    scaled = scaled_pool.tile([P, P], F32, name="scaled")
-                    nc.scalar.activation(scaled[:], by_token[:, (c - c0) * P:(c - c0 + 1) * P], ACT.Copy,
-                                         scale=gate_col[:, r, c:c + 1])
-                    nc.tensor.matmul(sums[c][:, 0:P], lhsT=scaled[:], rhs=ident[:], is_transpose=True,
-                                     start=(r == 0), stop=(r == TOP - 2))
-        last = fetched[TOP - 1]
-        for c0, c1 in FUSED_PIECES:
-            nc.vector.tensor_tensor(last[:, c0 * P:c1 * P], y[:].indirect(entries(pos_t[TOP - 1], c0 * P, c1 * P)),
-                                    gate_last[:, c0 * P:c1 * P], ALU.mult)
-        for c0, c1 in FUSED_PIECES:
-            for c in range(c0, c1):
-                nc.vector.tensor_tensor(result[:, c * P:(c + 1) * P], sums[c][:, 0:P], last[:, c * P:(c + 1) * P],
-                                        ALU.add)
-            nc.sync.dma_start(out=out[:, c0 * P:c1 * P], in_=result[:, c0 * P:c1 * P])
+        for r in range(TOP):
+            nc.vector.tensor_tensor(product[r][:], y[:].indirect(pos_t[r][:]), gate_t[r][:], ALU.mult)
+        for j in range(TOP // 2):
+            nc.vector.tensor_tensor(pair[j][:], product[2 * j][:], product[2 * j + 1][:], ALU.add)
+        for t0, t1 in STORE_PIECES:
+            nc.vector.tensor_tensor(result[:, t0:t1], pair[0][:, t0:t1], pair[1][:, t0:t1], ALU.add)
+            nc.sync.dma_start(out=out[:, t0:t1], in_=result[:, t0:t1])

@@ -13,8 +13,9 @@ PER_COL = 16
 FLOPS = 2 * S * (2 * K * H + H * N)
 BYTES = PASSES * T * (4 * P + 16) + E * (2 * PASSES * H + N) * (2 * P + 16) + 4 * TOP * T + 2 * P * (S + TOP * T) // PER_COL + 4 * N * T
 
-SCALE_RUNS = ((0, 4), (4, 6))
-STORE_PIECES = ((0, 384), (384, T))
+W3_RUNS = ((0, 3), (3, 6))
+BYTE_WINDOW = 1024
+TURNED_TOKENS = 384
 
 F32 = mybir.dt.float32
 BF16 = mybir.dt.bfloat16
@@ -28,10 +29,10 @@ ACT = mybir.ActivationFunctionType
 ALU = mybir.AluOpType
 
 
-def load_plane(nc, plane, rows):
+def load_plane(queue, plane, rows):
     by_row = rows.rearrange("g (q r) w -> r q g w", r=4)
     for r in range(4):
-        nc.sync.dma_start(
+        queue.dma_start(
             out=plane[r:P:32, :].bitcast(I32).rearrange("q (g w) -> q g w", g=rows.shape[0]),
             in_=by_row[r].bitcast(I32),
         )
@@ -59,128 +60,121 @@ def tile_moe_ecr_glu_relu_kernel(
     nc = tc.nc
     with ExitStack() as ctx:
         keep = ctx.enter_context(tc.tile_pool(name="keep", bufs=1))
-        ring = ctx.enter_context(tc.tile_pool(name="ring", bufs=2))
         psum = ctx.enter_context(tc.psum_pool(name="psum", bufs=1))
 
         def bank(b):
             return psum.tile([P, 512], F32, name="bank", tag="bank%d" % b)
 
-        x_plane = keep.tile([P, PASSES * T], U8, name="x_plane", align_bytes=64)
-        w1_planes = [keep.tile([P, (e1 - e0) * PASSES * H], U8, name="w1_plane%d" % e0, align_bytes=64)
-                     for e0, e1 in SCALE_RUNS]
+        x_plane = keep.tile([P, BYTE_WINDOW], U8, name="x_plane", align_bytes=64)
+        slot_planes = [keep.tile([P, S], U8, name="slot_plane%d" % s, align_bytes=64) for s in range(PASSES)]
+        w1_plane = keep.tile([P, E * PASSES * H], U8, name="w1_plane", align_bytes=64)
         w3_planes = [keep.tile([P, (e1 - e0) * PASSES * H], U8, name="w3_plane%d" % e0, align_bytes=64)
-                     for e0, e1 in SCALE_RUNS]
+                     for e0, e1 in W3_RUNS]
         w2_plane = keep.tile([P, E * N], U8, name="w2_plane", align_bytes=64)
         y = keep.tile([P, S + PAD], F32, name="y", align_bytes=64)
         ident = keep.tile([P, P], F32, name="ident")
-        nc.vector.memset(x_plane[:].bitcast(I32), 0)
-        nc.vector.memset(w1_planes[0][:].bitcast(I32), 0)
-        nc.gpsimd.memset(w3_planes[0][:].bitcast(I32), 0)
+        nc.gpsimd.memset(x_plane[:].bitcast(I32), 0)
+        for plane in (w1_plane, w3_planes[0], w3_planes[1]):
+            nc.vector.memset(plane[:].bitcast(I32), 0)
         make_identity(nc, ident[:])
+        nc.gpsimd.memset(slot_planes[1][:].bitcast(I32), 0)
         nc.gpsimd.memset(w2_plane[:].bitcast(I32), 0)
-        nc.vector.memset(w1_planes[1][:].bitcast(I32), 0)
-        nc.gpsimd.memset(w3_planes[1][:].bitcast(I32), 0)
 
         offs_t = keep.tile([P, S // PER_COL], U16, name="offs_t")
-        x_t = keep.tile([P, PASSES * T], I32, name="x_t", align_bytes=64)
-        w1_t = [keep.tile([P, PASSES * 2 * H], U8, name="w1_t%d" % e, align_bytes=64) for e in range(E)]
+        x_t = keep.tile([P, PASSES * T * 4], U8, name="x_t", align_bytes=64)
+        w1_t = [keep.tile([P, 2 * PASSES * 2 * H], U8, name="w1_t%d" % j, align_bytes=64) for j in range(E // 2)]
         w3_t = [keep.tile([P, PASSES * 2 * H], U8, name="w3_t%d" % e, align_bytes=64) for e in range(E)]
         w2_t = keep.tile([P, E * 2 * N], U8, name="w2_t", align_bytes=64)
         pos_t = [keep.tile([P, T // PER_COL], U16, name="pos_t%d" % r) for r in range(TOP)]
-        gate_t = [keep.tile([P, T], F32, name="gate_t%d" % r) for r in range(TOP)]
+        token_parts = ((0, TURNED_TOKENS), (TURNED_TOKENS, T))
+        gate_t = {t0: keep.tile([P, TOP * (t1 - t0)], F32, name="gate_t%d" % t0) for t0, t1 in token_parts}
 
         nc.sync.dma_start(offs_t[:], offs)
-        for s in range(PASSES):
-            nc.sync.dma_start(out=x_t[:, s * T:(s + 1) * T],
-                              in_=x_words[s].rearrange("p t r -> p (t r)").bitcast(I32))
-        load_plane(nc, x_plane, x_scales)
-        for run, (e0, e1) in enumerate(SCALE_RUNS):
+        for q in range(4):
+            nc.sync.dma_start(out=x_plane[32 * q:32 * q + 4 * PASSES, 0:T].bitcast(I32),
+                              in_=x_scales[:, 4 * q:4 * q + 4, :].bitcast(I32))
+        load_words(nc, x_t, x_words.rearrange("s p t r -> s p (t r)"))
+
+        def load_w1(j):
+            load_words(nc, w1_t[j], w1_words[2 * j:2 * j + 2].rearrange("e s p b -> (e s) p b"))
+
+        load_plane(nc.sync, w1_plane[:], w1_scales.rearrange("e s q w -> (e s) q w"))
+        load_w1(0)
+        nc.vector.tensor_copy(slot_planes[0][:], x_plane[:].indirect(offs_t[:]))
+        for r in range(4):
+            nc.sync.dma_start(out=slot_planes[1][r:P:32, :].bitcast(I32), in_=slot_planes[0][4 + r:P:32, :].bitcast(I32))
+        load_w1(1)
+        for run, (e0, e1) in enumerate(W3_RUNS):
+            load_plane(nc.sync, w3_planes[run][:], w3_scales[e0:e1].rearrange("e s q w -> (e s) q w"))
             for e in range(e0, e1):
-                for w_t, words, w_planes, scales in ((w1_t, w1_words, w1_planes, w1_scales),
-                                                     (w3_t, w3_words, w3_planes, w3_scales)):
-                    if e == e0:
-                        load_plane(nc, w_planes[run], scales[e0:e1].rearrange("e s q w -> (e s) q w"))
-                    load_words(nc, w_t[e], words[e])
-        load_plane(nc, w2_plane, w2_scales.rearrange("e s q w -> (e s) q w"))
+                load_words(nc, w3_t[e], w3_words[e])
+            if run == 0:
+                load_w1(2)
+        load_plane(nc.sync, w2_plane[:], w2_scales.rearrange("e s q w -> (e s) q w"))
         load_words(nc, w2_t, w2_words.rearrange("e s p b -> (e s) p b"))
         for r, pos in enumerate((pos1, pos2, pos3, pos4)):
             nc.sync.dma_start(pos_t[r][:], pos)
-        for r in range(TOP):
-            nc.sync.dma_start(out=gate_t[r][:], in_=gate[r])
+        for t0, t1 in token_parts:
+            nc.sync.dma_start(out=gate_t[t0][:].rearrange("n (r t) -> n r t", r=TOP),
+                              in_=gate[:, :, t0:t1].rearrange("r n t -> n r t"))
 
         nc.scalar.activation(y[:, S:S + PAD], ident[:, 0:PAD], ACT.Relu, scale=-1.0)
 
-        tokens = {}
+        slot_words = {}
+        for e0 in range(0, E, 2):
+            for s in range(PASSES):
+                words = keep.tile([P, 2 * C], U32, name="words%d%d" % (e0, s), align_bytes=64)
+                window = x_t[:].bitcast(U32)[:, s * T:(s + 1) * T]
+                nc.vector.tensor_copy(words[:], window.indirect(entries(offs_t, e0 * C, (e0 + 2) * C)))
+                for j in range(2):
+                    slot_words[e0 + j, s] = words[:, j * C:(j + 1) * C]
 
-        def gather_tokens(e0, e1, room):
-            offsets = entries(offs_t, e0 * C, e1 * C)
-            words = [keep.tile([P, (e1 - e0) * C], U32, name="words", tag="words%d%d" % (room, s), align_bytes=64)
-                     for s in range(PASSES)]
-            planes = [keep.tile([P, (e1 - e0) * C], U8, name="planes", tag="planes%d%d" % (room, s), align_bytes=64)
-                      for s in range(PASSES)]
+        def first_layer(dst, e, words, plane):
             for s in range(PASSES):
-                nc.vector.tensor_copy(words[s][:], x_t[:].bitcast(U32)[:, s * T:(s + 1) * T].indirect(offsets))
-            for s in range(PASSES):
-                nc.vector.tensor_copy(planes[s][:], x_plane[:, s * T:(s + 1) * T].indirect(offsets))
-            for e in range(e0, e1):
-                for s in range(PASSES):
-                    cols = slice((e - e0) * C, (e - e0 + 1) * C)
-                    tokens[e, s] = (words[s][:, cols], planes[s][:, cols])
-
-        def first_layer(dst, e, w_t, w_planes, i0, width):
-            run = [j for j, (e0, e1) in enumerate(SCALE_RUNS) if e0 <= e < e1][0]
-            for s in range(PASSES):
-                word0 = s * H + i0
-                byte0 = ((e - SCALE_RUNS[run][0]) * PASSES + s) * H + i0
                 nc.tensor.matmul_mx(
-                    out=dst,
-                    lhsT=tokens[e, s][0].bitcast(FP8X4), lhsT_scale=tokens[e, s][1],
-                    rhs=w_t[e][:, 2 * word0:2 * (word0 + width)].bitcast(FP4X4),
-                    rhs_scale=w_planes[run][:, byte0:byte0 + width],
+                    out=dst[:],
+                    lhsT=slot_words[e, s].bitcast(FP8X4), lhsT_scale=slot_planes[s][:, e * C:(e + 1) * C],
+                    rhs=words[:, 2 * s * H:2 * (s + 1) * H].bitcast(FP4X4),
+                    rhs_scale=plane[:, s * H:(s + 1) * H],
                     start=(s == 0), stop=(s == PASSES - 1),
                 )
 
         hidden, quantised = {}, {}
 
-        def turn(e, dst):
-            pairs = hidden[e][:].rearrange("c u p v -> c (u p v)").bitcast(F32)
-            for u in range(2):
-                nc.tensor.transpose(dst[:, u * P:(u + 1) * P], pairs[:, u * P:(u + 1) * P], ident[:])
+        relu_a = {}
+        expert_bytes = PASSES * H
 
-        def quantise(e, src):
-            turned = ring.tile([P, C, 2], F32, name="turned", align_bytes=64)
-            nc.scalar.copy(turned[:], src.rearrange("p (u c) -> p c u", u=2))
-            h_words = ring.tile([P, C], U32, name="h_words", align_bytes=64, bufs=E)
-            h_plane = ring.tile([P, C], U8, name="h_plane", align_bytes=64, bufs=E)
+        def gate_branch(e, dst):
+            j = e % 2
+            first_layer(dst, e, w1_t[e // 2][:, 2 * j * expert_bytes:2 * (j + 1) * expert_bytes],
+                        w1_plane[:, e * expert_bytes:(e + 1) * expert_bytes])
+            relu_a[e] = keep.tile([P, 2, P, 2], F32, name="relu_a%d" % e, align_bytes=64)
+            nc.scalar.activation(relu_a[e][:], by_pair(dst[:]), ACT.Relu)
+
+        def value_branch(e, dst):
+            j = e % 3
+            first_layer(dst, e, w3_t[e][:], w3_planes[e // 3][:, j * expert_bytes:(j + 1) * expert_bytes])
+            hidden[e] = keep.tile([P, 2, P, 2], BF16, name="h%d" % e, align_bytes=64)
+            nc.vector.tensor_tensor(hidden[e][:], by_pair(dst[:]), relu_a[e][:], ALU.mult)
+
+        def turn_and_quantise(e0, e1, room_bank):
+            n = e1 - e0
+            room = bank(room_bank)[:, 0:n * 2 * P]
+            for e in range(e0, e1):
+                pairs = hidden[e][:].rearrange("c u p v -> c (u p v)").bitcast(F32)
+                for u in range(2):
+                    col = ((e - e0) * 2 + u) * P
+                    nc.tensor.transpose(room[:, col:col + P], pairs[:, u * P:(u + 1) * P], ident[:])
+            turned = keep.tile([P, n, C, 2], F32, name="turned%d" % e0, align_bytes=64)
+            nc.scalar.copy(turned[:], room.rearrange("p (e u c) -> p e c u", e=n, u=2))
+            h_words = keep.tile([P, n * C], U32, name="h_words%d" % e0, align_bytes=64)
+            h_plane = keep.tile([P, n * C], U8, name="h_plane%d" % e0, align_bytes=64)
             nc.vector.quantize_mx(
                 out=h_words[:].bitcast(FP8X4), scales=h_plane[:],
-                in_=turned[:].rearrange("p c u -> p (c u)").bitcast(BF16),
+                in_=turned[:].rearrange("p e c u -> p (e c u)").bitcast(BF16),
             )
-            quantised[e] = (h_words, h_plane)
-
-        def expert(e, to_turn):
-            a = bank(e % 2)
-            first_layer(a[:], e, w1_t, w1_planes, 0, H)
-            relu_a = ring.tile([P, 2, P, 2], F32, name="relu_a")
-            nc.scalar.activation(relu_a[:], by_pair(a[:]), ACT.Relu)
-            h = ring.tile([P, 2, P, 2], BF16, name="h", align_bytes=64, bufs=3)
-            hidden[e] = h
-            if not to_turn:
-                b = bank(2 + e % 2)
-                first_layer(b[:], e, w3_t, w3_planes, 0, H)
-                nc.vector.tensor_tensor(h[:], by_pair(b[:]), relu_a[:], ALU.mult)
-                return
-            halves = [bank(2 + e % 2), bank(4 + e % 2)]
-            for j in range(4):
-                first_layer(halves[j // 2][:, (j % 2) * P:(j % 2 + 1) * P], e, w3_t, w3_planes, j * P, P)
-            free = [half[:, 2 * P:4 * P] for half in halves[2 - len(to_turn):]]
-            for earlier, room in zip(to_turn, free):
-                turn(earlier, room)
-            for j, half in enumerate(halves):
-                ps = slice(j * P // 2, (j + 1) * P // 2)
-                nc.vector.tensor_tensor(h[:, :, ps, :], by_pair(half[:, 0:2 * P]), relu_a[:, :, ps, :], ALU.mult)
-            for earlier, room in zip(to_turn, free):
-                quantise(earlier, room)
+            for j in range(n):
+                quantised[e0 + j] = (h_words[:, j * C:(j + 1) * C], h_plane[:, j * C:(j + 1) * C])
 
         def second_layer(e0, e1, dst):
             for e in range(e0, e1):
@@ -188,35 +182,56 @@ def tile_moe_ecr_glu_relu_kernel(
                     out=dst[:, (e - e0) * C:(e - e0 + 1) * C],
                     lhsT=w2_t[:, e * 2 * N:(e + 1) * 2 * N].bitcast(FP4X4),
                     lhsT_scale=w2_plane[:, e * N:(e + 1) * N],
-                    rhs=quantised[e][0][:].bitcast(FP8X4), rhs_scale=quantised[e][1][:],
+                    rhs=quantised[e][0].bitcast(FP8X4), rhs_scale=quantised[e][1],
                     start=True, stop=True,
                 )
             nc.scalar.copy(y[:, e0 * C:e1 * C], dst[:, 0:(e1 - e0) * C])
 
-        gather_tokens(0, 1, 0)
-        gather_tokens(1, 3, 1)
-        gather_tokens(3, 4, 2)
-        TURNS = ((), (), (0, 1), (), (2,), (3, 4))
-        for e in range(E):
-            expert(e, TURNS[e])
-            if e == 0:
-                gather_tokens(4, 5, 0)
-            if e == 2:
-                gather_tokens(5, 6, 1)
-        last_turn = bank(0)[:, 0:2 * P]
-        turn(E - 1, last_turn)
-        quantise(E - 1, last_turn)
-        second_layer(0, 3, bank(6))
-        second_layer(3, 5, bank(7))
-        second_layer(5, 6, bank(1))
+        for e in range(4):
+            gate_branch(e, bank(e % 2))
+        for e in range(3):
+            value_branch(e, bank(2 + e))
+        turn_and_quantise(0, 2, 5)
+        gate_branch(4, bank(0))
+        gate_branch(5, bank(1))
+        turn_and_quantise(2, 3, 6)
+        for e in range(3, E):
+            value_branch(e, bank(e - 1))
+        turn_and_quantise(3, 4, 5)
+        turn_and_quantise(4, 5, 6)
+        turn_and_quantise(5, 6, 0)
+        second_layer(0, 4, bank(4))
+        second_layer(4, 5, bank(1))
+        second_layer(5, 6, bank(7))
 
         product = [keep.tile([P, T], F32, name="product%d" % r) for r in range(TOP)]
-        pair = [keep.tile([P, T], F32, name="pair%d" % j) for j in range(TOP // 2)]
         result = keep.tile([P, T], F32, name="result")
+
+        def fetch(r, t0, t1):
+            nc.vector.tensor_tensor(product[r][:, t0:t1], y[:].indirect(entries(pos_t[r], t0, t1)),
+                                    gate_t[t0][:, r * (t1 - t0):(r + 1) * (t1 - t0)], ALU.mult)
+
+        chunks = TURNED_TOKENS // P
+        sums = [bank(c) for c in range(chunks)]
         for r in range(TOP):
-            nc.vector.tensor_tensor(product[r][:], y[:].indirect(pos_t[r][:]), gate_t[r][:], ALU.mult)
-        for j in range(TOP // 2):
-            nc.vector.tensor_tensor(pair[j][:], product[2 * j][:], product[2 * j + 1][:], ALU.add)
-        for t0, t1 in STORE_PIECES:
-            nc.vector.tensor_tensor(result[:, t0:t1], pair[0][:, t0:t1], pair[1][:, t0:t1], ALU.add)
-            nc.sync.dma_start(out=out[:, t0:t1], in_=result[:, t0:t1])
+            fetch(r, 0, TURNED_TOKENS)
+            for c in range(chunks):
+                nc.tensor.matmul(sums[c][:, 0:P], lhsT=product[r][:, c * P:(c + 1) * P], rhs=ident[:],
+                                 is_transpose=True, start=(r == 0), stop=(r == TOP - 1))
+        back = bank(chunks)
+        for c in range(chunks):
+            by_token = keep.tile([P, P], F32, name="by_token%d" % c)
+            nc.scalar.copy(by_token[:], sums[c][:, 0:P])
+            nc.tensor.transpose(back[:, c * P:(c + 1) * P], by_token[:], ident[:])
+        nc.scalar.copy(result[:, 0:TURNED_TOKENS], back[:, 0:TURNED_TOKENS])
+        nc.scalar.dma_start(out=out[:, 0:TURNED_TOKENS], in_=result[:, 0:TURNED_TOKENS])
+
+        rest = slice(TURNED_TOKENS, T)
+        partial = [keep.tile([P, T - TURNED_TOKENS], F32, name="partial%d" % j) for j in range(TOP - 2)]
+        for r in range(TOP - 1):
+            fetch(r, TURNED_TOKENS, T)
+        nc.vector.tensor_tensor(partial[0][:], product[0][:, rest], product[1][:, rest], ALU.add)
+        fetch(TOP - 1, TURNED_TOKENS, T)
+        nc.vector.tensor_tensor(partial[1][:], partial[0][:], product[2][:, rest], ALU.add)
+        nc.vector.tensor_tensor(result[:, rest], partial[1][:], product[3][:, rest], ALU.add)
+        nc.sync.dma_start(out=out[:, rest], in_=result[:, rest])

@@ -74,15 +74,17 @@ def tile_moe_ecr_glu_relu_kernel(
         y = keep.tile([P, S + PAD], F32, name="y", align_bytes=64)
         ident = keep.tile([P, P], F32, name="ident")
         nc.gpsimd.memset(x_plane[:].bitcast(I32), 0)
-        for plane in (w1_plane, w3_planes[0], w3_planes[1]):
-            nc.vector.memset(plane[:].bitcast(I32), 0)
+        half = 7 * H
+        nc.gpsimd.memset(w1_plane[:, 0:half].bitcast(I32), 0)
+        for plane in (w1_plane[:, half:], w3_planes[0][:], w3_planes[1][:]):
+            nc.vector.memset(plane.bitcast(I32), 0)
         make_identity(nc, ident[:])
         nc.gpsimd.memset(slot_planes[1][:].bitcast(I32), 0)
         nc.gpsimd.memset(w2_plane[:].bitcast(I32), 0)
 
         offs_t = keep.tile([P, S // PER_COL], U16, name="offs_t")
-        x_t = keep.tile([P, PASSES * T * 4], U8, name="x_t", align_bytes=64)
-        w1_t = [keep.tile([P, 2 * PASSES * 2 * H], U8, name="w1_t%d" % j, align_bytes=64) for j in range(E // 2)]
+        x_t = [keep.tile([P, T], I32, name="x_t%d" % s, align_bytes=64) for s in range(PASSES)]
+        w1_t = [keep.tile([P, PASSES * 2 * H], U8, name="w1_t%d" % e, align_bytes=64) for e in range(E)]
         w3_t = [keep.tile([P, PASSES * 2 * H], U8, name="w3_t%d" % e, align_bytes=64) for e in range(E)]
         w2_t = keep.tile([P, E * 2 * N], U8, name="w2_t", align_bytes=64)
         pos_t = [keep.tile([P, T // PER_COL], U16, name="pos_t%d" % r) for r in range(TOP)]
@@ -90,26 +92,28 @@ def tile_moe_ecr_glu_relu_kernel(
         gate_t = {t0: keep.tile([P, TOP * (t1 - t0)], F32, name="gate_t%d" % t0) for t0, t1 in token_parts}
 
         nc.sync.dma_start(offs_t[:], offs)
-        for q in range(4):
-            nc.sync.dma_start(out=x_plane[32 * q:32 * q + 4 * PASSES, 0:T].bitcast(I32),
-                              in_=x_scales[:, 4 * q:4 * q + 4, :].bitcast(I32))
-        load_words(nc, x_t, x_words.rearrange("s p t r -> s p (t r)"))
+        x_rows = x_scales.rearrange("s (q r) t -> r q s t", r=4)
+        for r in range(4):
+            nc.sync.dma_start(out=x_plane[r:P:16, 0:T].bitcast(I32), in_=x_rows[r].bitcast(I32))
 
-        def load_w1(j):
-            load_words(nc, w1_t[j], w1_words[2 * j:2 * j + 2].rearrange("e s p b -> (e s) p b"))
+        def load_tokens(s):
+            nc.sync.dma_start(out=x_t[s][:], in_=x_words[s].rearrange("p t r -> p (t r)").bitcast(I32))
 
+        load_tokens(0)
+        load_words(nc, w1_t[0], w1_words[0])
         load_plane(nc.sync, w1_plane[:], w1_scales.rearrange("e s q w -> (e s) q w"))
-        load_w1(0)
+        load_words(nc, w1_t[1], w1_words[1])
+        load_tokens(1)
+        load_words(nc, w1_t[2], w1_words[2])
         nc.vector.tensor_copy(slot_planes[0][:], x_plane[:].indirect(offs_t[:]))
         for r in range(4):
-            nc.sync.dma_start(out=slot_planes[1][r:P:32, :].bitcast(I32), in_=slot_planes[0][4 + r:P:32, :].bitcast(I32))
-        load_w1(1)
+            nc.sync.dma_start(out=slot_planes[1][r:P:32, :].bitcast(I32), in_=slot_planes[0][16 + r:P:32, :].bitcast(I32))
+        for e in range(3, E):
+            load_words(nc, w1_t[e], w1_words[e])
         for run, (e0, e1) in enumerate(W3_RUNS):
             load_plane(nc.sync, w3_planes[run][:], w3_scales[e0:e1].rearrange("e s q w -> (e s) q w"))
             for e in range(e0, e1):
                 load_words(nc, w3_t[e], w3_words[e])
-            if run == 0:
-                load_w1(2)
         load_plane(nc.sync, w2_plane[:], w2_scales.rearrange("e s q w -> (e s) q w"))
         load_words(nc, w2_t, w2_words.rearrange("e s p b -> (e s) p b"))
         for r, pos in enumerate((pos1, pos2, pos3, pos4)):
@@ -121,39 +125,37 @@ def tile_moe_ecr_glu_relu_kernel(
         nc.scalar.activation(y[:, S:S + PAD], ident[:, 0:PAD], ACT.Relu, scale=-1.0)
 
         slot_words = {}
-        for e0 in range(0, E, 2):
-            for s in range(PASSES):
-                words = keep.tile([P, 2 * C], U32, name="words%d%d" % (e0, s), align_bytes=64)
-                window = x_t[:].bitcast(U32)[:, s * T:(s + 1) * T]
-                nc.vector.tensor_copy(words[:], window.indirect(entries(offs_t, e0 * C, (e0 + 2) * C)))
-                for j in range(2):
-                    slot_words[e0 + j, s] = words[:, j * C:(j + 1) * C]
+        for e0, s in ((0, 0), (2, 0), (4, 0), (0, 1), (2, 1), (4, 1)):
+            words = keep.tile([P, 2 * C], U32, name="words%d%d" % (e0, s), align_bytes=64)
+            window = x_t[s][:].bitcast(U32)
+            nc.vector.tensor_copy(words[:], window.indirect(entries(offs_t, e0 * C, (e0 + 2) * C)))
+            for j in range(2):
+                slot_words[e0 + j, s] = words[:, j * C:(j + 1) * C]
 
-        def first_layer(dst, e, words, plane):
-            for s in range(PASSES):
-                nc.tensor.matmul_mx(
-                    out=dst[:],
-                    lhsT=slot_words[e, s].bitcast(FP8X4), lhsT_scale=slot_planes[s][:, e * C:(e + 1) * C],
-                    rhs=words[:, 2 * s * H:2 * (s + 1) * H].bitcast(FP4X4),
-                    rhs_scale=plane[:, s * H:(s + 1) * H],
-                    start=(s == 0), stop=(s == PASSES - 1),
-                )
+        def first_layer(dst, e, s, words, plane):
+            nc.tensor.matmul_mx(
+                out=dst[:],
+                lhsT=slot_words[e, s].bitcast(FP8X4), lhsT_scale=slot_planes[s][:, e * C:(e + 1) * C],
+                rhs=words[:, 2 * s * H:2 * (s + 1) * H].bitcast(FP4X4),
+                rhs_scale=plane[:, s * H:(s + 1) * H],
+                start=(s == 0), stop=(s == PASSES - 1),
+            )
 
         hidden, quantised = {}, {}
 
         relu_a = {}
         expert_bytes = PASSES * H
 
-        def gate_branch(e, dst):
-            j = e % 2
-            first_layer(dst, e, w1_t[e // 2][:, 2 * j * expert_bytes:2 * (j + 1) * expert_bytes],
-                        w1_plane[:, e * expert_bytes:(e + 1) * expert_bytes])
-            relu_a[e] = keep.tile([P, 2, P, 2], F32, name="relu_a%d" % e, align_bytes=64)
-            nc.scalar.activation(relu_a[e][:], by_pair(dst[:]), ACT.Relu)
+        def gate_pass(e, s, dst):
+            first_layer(dst, e, s, w1_t[e][:], w1_plane[:, e * expert_bytes:(e + 1) * expert_bytes])
+            if s == PASSES - 1:
+                relu_a[e] = keep.tile([P, 2, P, 2], F32, name="relu_a%d" % e, align_bytes=64)
+                nc.scalar.activation(relu_a[e][:], by_pair(dst[:]), ACT.Relu)
 
         def value_branch(e, dst):
             j = e % 3
-            first_layer(dst, e, w3_t[e][:], w3_planes[e // 3][:, j * expert_bytes:(j + 1) * expert_bytes])
+            for s in range(PASSES):
+                first_layer(dst, e, s, w3_t[e][:], w3_planes[e // 3][:, j * expert_bytes:(j + 1) * expert_bytes])
             hidden[e] = keep.tile([P, 2, P, 2], BF16, name="h%d" % e, align_bytes=64)
             nc.vector.tensor_tensor(hidden[e][:], by_pair(dst[:]), relu_a[e][:], ALU.mult)
 
@@ -187,22 +189,27 @@ def tile_moe_ecr_glu_relu_kernel(
                 )
             nc.scalar.copy(y[:, e0 * C:e1 * C], dst[:, 0:(e1 - e0) * C])
 
-        for e in range(4):
-            gate_branch(e, bank(e % 2))
+        first_banks = [bank(b) for b in (0, 1, 6)]
+        for s in range(PASSES):
+            for e in range(3):
+                gate_pass(e, s, first_banks[e])
+        for e, b in ((3, 7), (4, 0), (5, 1)):
+            a = bank(b)
+            for s in range(PASSES):
+                gate_pass(e, s, a)
         for e in range(3):
             value_branch(e, bank(2 + e))
-        turn_and_quantise(0, 2, 5)
-        gate_branch(4, bank(0))
-        gate_branch(5, bank(1))
-        turn_and_quantise(2, 3, 6)
-        for e in range(3, E):
-            value_branch(e, bank(e - 1))
-        turn_and_quantise(3, 4, 5)
-        turn_and_quantise(4, 5, 6)
-        turn_and_quantise(5, 6, 0)
-        second_layer(0, 4, bank(4))
-        second_layer(4, 5, bank(1))
-        second_layer(5, 6, bank(7))
+        value_branch(3, bank(5))
+        turn_and_quantise(0, 2, 2)
+        value_branch(4, bank(7))
+        turn_and_quantise(2, 3, 3)
+        value_branch(5, bank(6))
+        turn_and_quantise(3, 4, 0)
+        turn_and_quantise(4, 5, 1)
+        turn_and_quantise(5, 6, 4)
+        second_layer(0, 4, bank(6))
+        second_layer(4, 5, bank(2))
+        second_layer(5, 6, bank(5))
 
         product = [keep.tile([P, T], F32, name="product%d" % r) for r in range(TOP)]
         result = keep.tile([P, T], F32, name="result")

@@ -14,7 +14,9 @@ FLOPS = 2 * S * (2 * K * H + H * N)
 BYTES = PASSES * T * (4 * P + 16) + E * (2 * PASSES * H + N) * (2 * P + 16) + 4 * TOP * T + 2 * P * (S + TOP * T) // PER_COL + 4 * N * T
 
 W3_RUNS = ((0, 3), (3, 6))
-BYTE_WINDOW = 1024
+BYTE_WINDOW = 1152
+ROOM = 4 * 2 * C
+X_PLANE_AT = ROOM - 64
 TURNED_TOKENS = 384
 
 F32 = mybir.dt.float32
@@ -60,12 +62,13 @@ def tile_moe_ecr_glu_relu_kernel(
     nc = tc.nc
     with ExitStack() as ctx:
         keep = ctx.enter_context(tc.tile_pool(name="keep", bufs=1))
+        reused = ctx.enter_context(tc.tile_pool(name="reused", bufs=1))
         psum = ctx.enter_context(tc.psum_pool(name="psum", bufs=1))
 
         def bank(b):
             return psum.tile([P, 512], F32, name="bank", tag="bank%d" % b)
 
-        x_plane = keep.tile([P, BYTE_WINDOW], U8, name="x_plane", align_bytes=64)
+        x_plane = reused.tile([P, BYTE_WINDOW], U8, name="x_plane", align_bytes=64, offset=X_PLANE_AT)
         slot_planes = [keep.tile([P, S], U8, name="slot_plane%d" % s, align_bytes=64) for s in range(PASSES)]
         w1_plane = keep.tile([P, E * PASSES * H], U8, name="w1_plane", align_bytes=64)
         w3_planes = [keep.tile([P, (e1 - e0) * PASSES * H], U8, name="w3_plane%d" % e0, align_bytes=64)
@@ -91,18 +94,17 @@ def tile_moe_ecr_glu_relu_kernel(
         token_parts = ((0, TURNED_TOKENS), (TURNED_TOKENS, T))
         gate_t = {t0: keep.tile([P, TOP * (t1 - t0)], F32, name="gate_t%d" % t0) for t0, t1 in token_parts}
 
-        nc.sync.dma_start(offs_t[:], offs)
-        x_rows = x_scales.rearrange("s (q r) t -> r q s t", r=4)
-        for r in range(4):
-            nc.sync.dma_start(out=x_plane[r:P:16, 0:T].bitcast(I32), in_=x_rows[r].bitcast(I32))
-
         def load_tokens(s):
             nc.sync.dma_start(out=x_t[s][:], in_=x_words[s].rearrange("p t r -> p (t r)").bitcast(I32))
 
         load_tokens(0)
-        load_words(nc, w1_t[0], w1_words[0])
+        nc.sync.dma_start(offs_t[:], offs)
+        x_rows = x_scales.rearrange("s (q r) t -> r q s t", r=4)
+        for r in range(4):
+            nc.sync.dma_start(out=x_plane[r:P:16, 0:T].bitcast(I32), in_=x_rows[r].bitcast(I32))
+        for e in (0, 1):
+            load_words(nc, w1_t[e], w1_words[e])
         load_plane(nc.sync, w1_plane[:], w1_scales.rearrange("e s q w -> (e s) q w"))
-        load_words(nc, w1_t[1], w1_words[1])
         load_tokens(1)
         load_words(nc, w1_t[2], w1_words[2])
         nc.vector.tensor_copy(slot_planes[0][:], x_plane[:].indirect(offs_t[:]))
@@ -113,7 +115,8 @@ def tile_moe_ecr_glu_relu_kernel(
         for run, (e0, e1) in enumerate(W3_RUNS):
             load_plane(nc.sync, w3_planes[run][:], w3_scales[e0:e1].rearrange("e s q w -> (e s) q w"))
             for e in range(e0, e1):
-                load_words(nc, w3_t[e], w3_words[e])
+                for s0, s1 in ((0, PASSES),) if e < E - 1 else ((0, 1), (1, PASSES)):
+                    load_words(nc, w3_t[e][:, 2 * H * s0:2 * H * s1], w3_words[e, s0:s1])
         load_plane(nc.sync, w2_plane[:], w2_scales.rearrange("e s q w -> (e s) q w"))
         load_words(nc, w2_t, w2_words.rearrange("e s p b -> (e s) p b"))
         for r, pos in enumerate((pos1, pos2, pos3, pos4)):
@@ -125,8 +128,11 @@ def tile_moe_ecr_glu_relu_kernel(
         nc.scalar.activation(y[:, S:S + PAD], ident[:, 0:PAD], ACT.Relu, scale=-1.0)
 
         slot_words = {}
-        for e0, s in ((0, 0), (2, 0), (4, 0), (0, 1), (2, 1), (4, 1)):
-            words = keep.tile([P, 2 * C], U32, name="words%d%d" % (e0, s), align_bytes=64)
+        for e0, s in ((0, 0), (2, 0), (0, 1), (2, 1), (4, 0), (4, 1)):
+            if s == 0:
+                words = reused.tile([P, 2 * C], U32, name="words%d%d" % (e0, s), align_bytes=64, offset=e0 // 2 * ROOM)
+            else:
+                words = keep.tile([P, 2 * C], U32, name="words%d%d" % (e0, s), align_bytes=64)
             window = x_t[s][:].bitcast(U32)
             nc.vector.tensor_copy(words[:], window.indirect(entries(offs_t, e0 * C, (e0 + 2) * C)))
             for j in range(2):
@@ -157,7 +163,8 @@ def tile_moe_ecr_glu_relu_kernel(
             for s in range(PASSES):
                 first_layer(dst, e, s, w3_t[e][:], w3_planes[e // 3][:, j * expert_bytes:(j + 1) * expert_bytes])
             hidden[e] = keep.tile([P, 2, P, 2], BF16, name="h%d" % e, align_bytes=64)
-            nc.vector.tensor_tensor(hidden[e][:], by_pair(dst[:]), relu_a[e][:], ALU.mult)
+            for u0, u1 in ((0, 2),) if e < E - 1 else ((0, 1), (1, 2)):
+                nc.vector.tensor_tensor(hidden[e][:, u0:u1], by_pair(dst[:])[:, u0:u1], relu_a[e][:, u0:u1], ALU.mult)
 
         def turn_and_quantise(e0, e1, room_bank):
             n = e1 - e0

@@ -115,15 +115,18 @@ def tile_moe_ecr_glu_relu_kernel(
         for run, (e0, e1) in enumerate(W3_RUNS):
             load_plane(nc.sync, w3_planes[run][:], w3_scales[e0:e1].rearrange("e s q w -> (e s) q w"))
             for e in range(e0, e1):
-                for s0, s1 in ((0, PASSES),) if e < E - 1 else ((0, 1), (1, PASSES)):
-                    load_words(nc, w3_t[e][:, 2 * H * s0:2 * H * s1], w3_words[e, s0:s1])
+                load_words(nc, w3_t[e], w3_words[e])
         load_plane(nc.sync, w2_plane[:], w2_scales.rearrange("e s q w -> (e s) q w"))
         load_words(nc, w2_t, w2_words.rearrange("e s p b -> (e s) p b"))
-        for r, pos in enumerate((pos1, pos2, pos3, pos4)):
-            nc.sync.dma_start(pos_t[r][:], pos)
-        for t0, t1 in token_parts:
+
+        def load_gate(t0, t1):
             nc.sync.dma_start(out=gate_t[t0][:].rearrange("n (r t) -> n r t", r=TOP),
                               in_=gate[:, :, t0:t1].rearrange("r n t -> n r t"))
+
+        load_gate(*token_parts[0])
+        for r, pos in enumerate((pos1, pos2, pos3, pos4)):
+            nc.sync.dma_start(pos_t[r][:], pos)
+        load_gate(*token_parts[1])
 
         nc.scalar.activation(y[:, S:S + PAD], ident[:, 0:PAD], ACT.Relu, scale=-1.0)
 

@@ -13,7 +13,7 @@ PER_COL = 16
 FLOPS = 2 * S * (2 * K * H + H * N)
 BYTES = PASSES * T * (4 * P + 16) + E * (2 * PASSES * H + N) * (2 * P + 16) + 4 * TOP * T + 2 * P * (S + TOP * T) // PER_COL + 4 * N * T
 
-W3_RUNS = ((0, 3), (3, 6))
+SCALE_RUNS = ((0, 3), (3, 6))
 BYTE_WINDOW = 1152
 ROOM = 4 * 2 * C
 X_PLANE_AT = ROOM - 64
@@ -70,17 +70,17 @@ def tile_moe_ecr_glu_relu_kernel(
 
         x_plane = reused.tile([P, BYTE_WINDOW], U8, name="x_plane", align_bytes=64, offset=X_PLANE_AT)
         slot_planes = [keep.tile([P, S], U8, name="slot_plane%d" % s, align_bytes=64) for s in range(PASSES)]
-        w1_plane = keep.tile([P, E * PASSES * H], U8, name="w1_plane", align_bytes=64)
+        w1_planes = [keep.tile([P, (e1 - e0) * PASSES * H], U8, name="w1_plane%d" % e0, align_bytes=64)
+                     for e0, e1 in SCALE_RUNS]
         w3_planes = [keep.tile([P, (e1 - e0) * PASSES * H], U8, name="w3_plane%d" % e0, align_bytes=64)
-                     for e0, e1 in W3_RUNS]
+                     for e0, e1 in SCALE_RUNS]
         w2_plane = keep.tile([P, E * N], U8, name="w2_plane", align_bytes=64)
         y = keep.tile([P, S + PAD], F32, name="y", align_bytes=64)
         ident = keep.tile([P, P], F32, name="ident")
         nc.gpsimd.memset(x_plane[:].bitcast(I32), 0)
-        half = 7 * H
-        nc.gpsimd.memset(w1_plane[:, 0:half].bitcast(I32), 0)
-        for plane in (w1_plane[:, half:], w3_planes[0][:], w3_planes[1][:]):
-            nc.vector.memset(plane.bitcast(I32), 0)
+        nc.gpsimd.memset(w1_planes[1][:].bitcast(I32), 0)
+        for plane in (w1_planes[0], w3_planes[0], w3_planes[1]):
+            nc.vector.memset(plane[:].bitcast(I32), 0)
         make_identity(nc, ident[:])
         nc.gpsimd.memset(slot_planes[1][:].bitcast(I32), 0)
         nc.gpsimd.memset(w2_plane[:].bitcast(I32), 0)
@@ -102,31 +102,50 @@ def tile_moe_ecr_glu_relu_kernel(
         x_rows = x_scales.rearrange("s (q r) t -> r q s t", r=4)
         for r in range(4):
             nc.sync.dma_start(out=x_plane[r:P:16, 0:T].bitcast(I32), in_=x_rows[r].bitcast(I32))
-        for e in (0, 1):
+
+        def load_rows(planes, scales, run):
+            e0, e1 = SCALE_RUNS[run]
+            load_plane(nc.sync, planes[run][:], scales[e0:e1].rearrange("e s q w -> (e s) q w"))
+
+        def load_w1(e):
             load_words(nc, w1_t[e], w1_words[e])
-        load_plane(nc.sync, w1_plane[:], w1_scales.rearrange("e s q w -> (e s) q w"))
+
+        def load_w3(e):
+            load_words(nc, w3_t[e], w3_words[e])
+
+        load_w1(0)
+        load_rows(w1_planes, w1_scales, 0)
+        load_w1(1)
         load_tokens(1)
-        load_words(nc, w1_t[2], w1_words[2])
+        load_w1(2)
         nc.vector.tensor_copy(slot_planes[0][:], x_plane[:].indirect(offs_t[:]))
         for r in range(4):
             nc.sync.dma_start(out=slot_planes[1][r:P:32, :].bitcast(I32), in_=slot_planes[0][16 + r:P:32, :].bitcast(I32))
-        for e in range(3, E):
-            load_words(nc, w1_t[e], w1_words[e])
-        for run, (e0, e1) in enumerate(W3_RUNS):
-            load_plane(nc.sync, w3_planes[run][:], w3_scales[e0:e1].rearrange("e s q w -> (e s) q w"))
-            for e in range(e0, e1):
-                load_words(nc, w3_t[e], w3_words[e])
+        load_w1(3)
+        load_w1(4)
+        load_rows(w1_planes, w1_scales, 1)
+        load_w3(0)
+        load_w3(1)
+        load_rows(w3_planes, w3_scales, 0)
+        load_w3(2)
+        load_w1(5)
+        load_w3(3)
+        load_rows(w3_planes, w3_scales, 1)
+        load_w3(4)
+        load_w3(5)
         load_plane(nc.sync, w2_plane[:], w2_scales.rearrange("e s q w -> (e s) q w"))
         load_words(nc, w2_t, w2_words.rearrange("e s p b -> (e s) p b"))
 
-        def load_gate(t0, t1):
-            nc.sync.dma_start(out=gate_t[t0][:].rearrange("n (r t) -> n r t", r=TOP),
-                              in_=gate[:, :, t0:t1].rearrange("r n t -> n r t"))
+        def load_gate(part, r0, r1):
+            t0, t1 = token_parts[part]
+            nc.sync.dma_start(out=gate_t[t0][:].rearrange("n (r t) -> n r t", r=TOP)[:, r0:r1, :],
+                              in_=gate[r0:r1, :, t0:t1].rearrange("r n t -> n r t"))
 
-        load_gate(*token_parts[0])
-        for r, pos in enumerate((pos1, pos2, pos3, pos4)):
-            nc.sync.dma_start(pos_t[r][:], pos)
-        load_gate(*token_parts[1])
+        for r0, lists in ((0, (pos1, pos2)), (2, (pos3, pos4))):
+            load_gate(0, r0, r0 + 2)
+            for j, pos in enumerate(lists):
+                nc.sync.dma_start(pos_t[r0 + j][:], pos)
+        load_gate(1, 0, TOP)
 
         nc.scalar.activation(y[:, S:S + PAD], ident[:, 0:PAD], ACT.Relu, scale=-1.0)
 
@@ -156,7 +175,8 @@ def tile_moe_ecr_glu_relu_kernel(
         expert_bytes = PASSES * H
 
         def gate_pass(e, s, dst):
-            first_layer(dst, e, s, w1_t[e][:], w1_plane[:, e * expert_bytes:(e + 1) * expert_bytes])
+            j = e % 3
+            first_layer(dst, e, s, w1_t[e][:], w1_planes[e // 3][:, j * expert_bytes:(j + 1) * expert_bytes])
             if s == PASSES - 1:
                 relu_a[e] = keep.tile([P, 2, P, 2], F32, name="relu_a%d" % e, align_bytes=64)
                 nc.scalar.activation(relu_a[e][:], by_pair(dst[:]), ACT.Relu)
@@ -203,12 +223,16 @@ def tile_moe_ecr_glu_relu_kernel(
         for s in range(PASSES):
             for e in range(3):
                 gate_pass(e, s, first_banks[e])
-        for e, b in ((3, 7), (4, 0), (5, 1)):
-            a = bank(b)
+
+        def gate_branch(e, dst):
             for s in range(PASSES):
-                gate_pass(e, s, a)
+                gate_pass(e, s, dst)
+
+        gate_branch(3, bank(7))
+        gate_branch(4, bank(0))
         for e in range(3):
             value_branch(e, bank(2 + e))
+        gate_branch(5, bank(1))
         value_branch(3, bank(5))
         turn_and_quantise(0, 2, 2)
         value_branch(4, bank(7))
@@ -244,11 +268,14 @@ def tile_moe_ecr_glu_relu_kernel(
         nc.scalar.dma_start(out=out[:, 0:TURNED_TOKENS], in_=result[:, 0:TURNED_TOKENS])
 
         rest = slice(TURNED_TOKENS, T)
-        partial = [keep.tile([P, T - TURNED_TOKENS], F32, name="partial%d" % j) for j in range(TOP - 2)]
+        partial = [keep.tile([P, T], F32, name="partial%d" % j) for j in range(TOP - 2)]
         for r in range(TOP - 1):
             fetch(r, TURNED_TOKENS, T)
-        nc.vector.tensor_tensor(partial[0][:], product[0][:, rest], product[1][:, rest], ALU.add)
+        nc.vector.tensor_tensor(partial[0][:, rest], product[0][:, rest], product[1][:, rest], ALU.add)
         fetch(TOP - 1, TURNED_TOKENS, T)
-        nc.vector.tensor_tensor(partial[1][:], partial[0][:], product[2][:, rest], ALU.add)
-        nc.vector.tensor_tensor(result[:, rest], partial[1][:], product[3][:, rest], ALU.add)
-        nc.sync.dma_start(out=out[:, rest], in_=result[:, rest])
+        last_chunks = [slice(t0, t0 + P) for t0 in range(TURNED_TOKENS, T, P)]
+        for ts in last_chunks:
+            nc.vector.tensor_tensor(partial[1][:, ts], partial[0][:, ts], product[2][:, ts], ALU.add)
+        for ts, queue in zip(last_chunks, (nc.scalar, nc.sync)):
+            nc.vector.tensor_tensor(result[:, ts], partial[1][:, ts], product[3][:, ts], ALU.add)
+            queue.dma_start(out=out[:, ts], in_=result[:, ts])

@@ -13,10 +13,9 @@ PER_COL = 16
 FLOPS = 2 * S * (2 * K * H + H * N)
 BYTES = PASSES * T * (4 * P + 16) + E * (2 * PASSES * H + N) * (2 * P + 16) + 4 * TOP * T + 2 * P * (S + TOP * T) // PER_COL + 4 * N * T
 
-SCALE_RUNS = ((0, 3), (3, 6))
-BYTE_WINDOW = 1152
-ROOM = 4 * 2 * C
-X_PLANE_AT = ROOM - 64
+W1_RUNS = ((0, 4), (4, 6))
+W3_RUNS = ((0, 3), (3, 6))
+BYTE_WINDOW = 1024
 TURNED_TOKENS = 384
 
 F32 = mybir.dt.float32
@@ -62,27 +61,29 @@ def tile_moe_ecr_glu_relu_kernel(
     nc = tc.nc
     with ExitStack() as ctx:
         keep = ctx.enter_context(tc.tile_pool(name="keep", bufs=1))
-        reused = ctx.enter_context(tc.tile_pool(name="reused", bufs=1))
         psum = ctx.enter_context(tc.psum_pool(name="psum", bufs=1))
 
         def bank(b):
             return psum.tile([P, 512], F32, name="bank", tag="bank%d" % b)
 
-        x_plane = reused.tile([P, BYTE_WINDOW], U8, name="x_plane", align_bytes=64, offset=X_PLANE_AT)
+        x_plane = keep.tile([P, BYTE_WINDOW], U8, name="x_plane", align_bytes=64)
         slot_planes = [keep.tile([P, S], U8, name="slot_plane%d" % s, align_bytes=64) for s in range(PASSES)]
         w1_planes = [keep.tile([P, (e1 - e0) * PASSES * H], U8, name="w1_plane%d" % e0, align_bytes=64)
-                     for e0, e1 in SCALE_RUNS]
+                     for e0, e1 in W1_RUNS]
         w3_planes = [keep.tile([P, (e1 - e0) * PASSES * H], U8, name="w3_plane%d" % e0, align_bytes=64)
-                     for e0, e1 in SCALE_RUNS]
+                     for e0, e1 in W3_RUNS]
         w2_plane = keep.tile([P, E * N], U8, name="w2_plane", align_bytes=64)
         y = keep.tile([P, S + PAD], F32, name="y", align_bytes=64)
         ident = keep.tile([P, P], F32, name="ident")
-        nc.gpsimd.memset(x_plane[:].bitcast(I32), 0)
-        nc.gpsimd.memset(w1_planes[1][:].bitcast(I32), 0)
-        for plane in (w1_planes[0], w3_planes[0], w3_planes[1]):
-            nc.vector.memset(plane[:].bitcast(I32), 0)
+        nc.gpsimd.memset(x_plane[:, 0:T].bitcast(I32), 0)
+        half = W1_RUNS[0][1] * PASSES * H // 2
+        nc.gpsimd.memset(w1_planes[0][:, 0:half].bitcast(I32), 0)
+        for plane in (w1_planes[0][:, half:], w3_planes[0][:], w3_planes[1][:]):
+            nc.vector.memset(plane.bitcast(I32), 0)
+        nc.gpsimd.memset(x_plane[:, T:].bitcast(I32), 0)
         make_identity(nc, ident[:])
         nc.gpsimd.memset(slot_planes[1][:].bitcast(I32), 0)
+        nc.gpsimd.memset(w1_planes[1][:].bitcast(I32), 0)
         nc.gpsimd.memset(w2_plane[:].bitcast(I32), 0)
 
         offs_t = keep.tile([P, S // PER_COL], U16, name="offs_t")
@@ -97,14 +98,13 @@ def tile_moe_ecr_glu_relu_kernel(
         def load_tokens(s):
             nc.sync.dma_start(out=x_t[s][:], in_=x_words[s].rearrange("p t r -> p (t r)").bitcast(I32))
 
-        load_tokens(0)
         nc.sync.dma_start(offs_t[:], offs)
         x_rows = x_scales.rearrange("s (q r) t -> r q s t", r=4)
         for r in range(4):
             nc.sync.dma_start(out=x_plane[r:P:16, 0:T].bitcast(I32), in_=x_rows[r].bitcast(I32))
 
-        def load_rows(planes, scales, run):
-            e0, e1 = SCALE_RUNS[run]
+        def load_rows(planes, scales, runs, run):
+            e0, e1 = runs[run]
             load_plane(nc.sync, planes[run][:], scales[e0:e1].rearrange("e s q w -> (e s) q w"))
 
         def load_w1(e):
@@ -113,24 +113,24 @@ def tile_moe_ecr_glu_relu_kernel(
         def load_w3(e):
             load_words(nc, w3_t[e], w3_words[e])
 
+        load_tokens(0)
         load_w1(0)
-        load_rows(w1_planes, w1_scales, 0)
-        load_w1(1)
+        load_rows(w1_planes, w1_scales, W1_RUNS, 0)
         load_tokens(1)
-        load_w1(2)
+        for e in (1, 2, 3):
+            load_w1(e)
         nc.vector.tensor_copy(slot_planes[0][:], x_plane[:].indirect(offs_t[:]))
         for r in range(4):
             nc.sync.dma_start(out=slot_planes[1][r:P:32, :].bitcast(I32), in_=slot_planes[0][16 + r:P:32, :].bitcast(I32))
-        load_w1(3)
-        load_w1(4)
-        load_rows(w1_planes, w1_scales, 1)
         load_w3(0)
+        load_rows(w3_planes, w3_scales, W3_RUNS, 0)
         load_w3(1)
-        load_rows(w3_planes, w3_scales, 0)
         load_w3(2)
+        load_w1(4)
+        load_rows(w1_planes, w1_scales, W1_RUNS, 1)
         load_w1(5)
         load_w3(3)
-        load_rows(w3_planes, w3_scales, 1)
+        load_rows(w3_planes, w3_scales, W3_RUNS, 1)
         load_w3(4)
         load_w3(5)
         load_plane(nc.sync, w2_plane[:], w2_scales.rearrange("e s q w -> (e s) q w"))
@@ -151,10 +151,7 @@ def tile_moe_ecr_glu_relu_kernel(
 
         slot_words = {}
         for e0, s in ((0, 0), (2, 0), (0, 1), (2, 1), (4, 0), (4, 1)):
-            if s == 0:
-                words = reused.tile([P, 2 * C], U32, name="words%d%d" % (e0, s), align_bytes=64, offset=e0 // 2 * ROOM)
-            else:
-                words = keep.tile([P, 2 * C], U32, name="words%d%d" % (e0, s), align_bytes=64)
+            words = keep.tile([P, 2 * C], U32, name="words%d%d" % (e0, s), align_bytes=64)
             window = x_t[s][:].bitcast(U32)
             nc.vector.tensor_copy(words[:], window.indirect(entries(offs_t, e0 * C, (e0 + 2) * C)))
             for j in range(2):
@@ -175,8 +172,9 @@ def tile_moe_ecr_glu_relu_kernel(
         expert_bytes = PASSES * H
 
         def gate_pass(e, s, dst):
-            j = e % 3
-            first_layer(dst, e, s, w1_t[e][:], w1_planes[e // 3][:, j * expert_bytes:(j + 1) * expert_bytes])
+            run = 0 if e < W1_RUNS[0][1] else 1
+            j = e - W1_RUNS[run][0]
+            first_layer(dst, e, s, w1_t[e][:], w1_planes[run][:, j * expert_bytes:(j + 1) * expert_bytes])
             if s == PASSES - 1:
                 relu_a[e] = keep.tile([P, 2, P, 2], F32, name="relu_a%d" % e, align_bytes=64)
                 nc.scalar.activation(relu_a[e][:], by_pair(dst[:]), ACT.Relu)
@@ -219,24 +217,23 @@ def tile_moe_ecr_glu_relu_kernel(
                 )
             nc.scalar.copy(y[:, e0 * C:e1 * C], dst[:, 0:(e1 - e0) * C])
 
-        first_banks = [bank(b) for b in (0, 1, 6)]
+        first_banks = [bank(b) for b in (0, 1, 6, 7)]
         for s in range(PASSES):
-            for e in range(3):
+            for e in range(4):
                 gate_pass(e, s, first_banks[e])
 
         def gate_branch(e, dst):
             for s in range(PASSES):
                 gate_pass(e, s, dst)
 
-        gate_branch(3, bank(7))
-        gate_branch(4, bank(0))
         for e in range(3):
             value_branch(e, bank(2 + e))
-        gate_branch(5, bank(1))
-        value_branch(3, bank(5))
+        gate_branch(4, bank(0))
         turn_and_quantise(0, 2, 2)
-        value_branch(4, bank(7))
+        gate_branch(5, bank(1))
         turn_and_quantise(2, 3, 3)
+        value_branch(3, bank(5))
+        value_branch(4, bank(7))
         value_branch(5, bank(6))
         turn_and_quantise(3, 4, 0)
         turn_and_quantise(4, 5, 1)

@@ -13,8 +13,7 @@ PER_COL = 16
 FLOPS = 2 * S * (2 * K * H + H * N)
 BYTES = PASSES * T * (4 * P + 16) + E * (2 * PASSES * H + N) * (2 * P + 16) + 4 * TOP * T + 2 * P * (S + TOP * T) // PER_COL + 4 * N * T
 
-W1_RUNS = ((0, 4), (4, 6))
-W3_RUNS = ((0, 3), (3, 6))
+GROUP = 3
 BYTE_WINDOW = 1024
 TURNED_TOKENS = 384
 
@@ -66,24 +65,23 @@ def tile_moe_ecr_glu_relu_kernel(
         def bank(b):
             return psum.tile([P, 512], F32, name="bank", tag="bank%d" % b)
 
-        x_plane = keep.tile([P, BYTE_WINDOW], U8, name="x_plane", align_bytes=64)
+        shared = ctx.enter_context(tc.tile_pool(name="shared", bufs=1))
+        x_plane = shared.tile([P, BYTE_WINDOW], U8, name="x_plane", align_bytes=64, offset=BYTE_WINDOW // 2)
         slot_planes = [keep.tile([P, S], U8, name="slot_plane%d" % s, align_bytes=64) for s in range(PASSES)]
-        w1_planes = [keep.tile([P, (e1 - e0) * PASSES * H], U8, name="w1_plane%d" % e0, align_bytes=64)
-                     for e0, e1 in W1_RUNS]
-        w3_planes = [keep.tile([P, (e1 - e0) * PASSES * H], U8, name="w3_plane%d" % e0, align_bytes=64)
-                     for e0, e1 in W3_RUNS]
+        expert_bytes = PASSES * H
+        w1_planes = [keep.tile([P, GROUP * expert_bytes], U8, name="w1_plane%d" % g, align_bytes=64) for g in range(2)]
+        w3_planes = [keep.tile([P, GROUP * expert_bytes], U8, name="w3_plane%d" % g, align_bytes=64) for g in range(2)]
         w2_plane = keep.tile([P, E * N], U8, name="w2_plane", align_bytes=64)
         y = keep.tile([P, S + PAD], F32, name="y", align_bytes=64)
         ident = keep.tile([P, P], F32, name="ident")
         nc.gpsimd.memset(x_plane[:, 0:T].bitcast(I32), 0)
-        half = W1_RUNS[0][1] * PASSES * H // 2
-        nc.gpsimd.memset(w1_planes[0][:, 0:half].bitcast(I32), 0)
-        for plane in (w1_planes[0][:, half:], w3_planes[0][:], w3_planes[1][:]):
-            nc.vector.memset(plane.bitcast(I32), 0)
+        nc.gpsimd.memset(w1_planes[0][:].bitcast(I32), 0)
+        nc.vector.memset(w3_planes[0][:].bitcast(I32), 0)
+        nc.vector.memset(w1_planes[1][:].bitcast(I32), 0)
         nc.gpsimd.memset(x_plane[:, T:].bitcast(I32), 0)
         make_identity(nc, ident[:])
         nc.gpsimd.memset(slot_planes[1][:].bitcast(I32), 0)
-        nc.gpsimd.memset(w1_planes[1][:].bitcast(I32), 0)
+        nc.gpsimd.memset(w3_planes[1][:].bitcast(I32), 0)
         nc.gpsimd.memset(w2_plane[:].bitcast(I32), 0)
 
         offs_t = keep.tile([P, S // PER_COL], U16, name="offs_t")
@@ -98,14 +96,9 @@ def tile_moe_ecr_glu_relu_kernel(
         def load_tokens(s):
             nc.sync.dma_start(out=x_t[s][:], in_=x_words[s].rearrange("p t r -> p (t r)").bitcast(I32))
 
-        nc.sync.dma_start(offs_t[:], offs)
-        x_rows = x_scales.rearrange("s (q r) t -> r q s t", r=4)
-        for r in range(4):
-            nc.sync.dma_start(out=x_plane[r:P:16, 0:T].bitcast(I32), in_=x_rows[r].bitcast(I32))
-
-        def load_rows(planes, scales, runs, run):
-            e0, e1 = runs[run]
-            load_plane(nc.sync, planes[run][:], scales[e0:e1].rearrange("e s q w -> (e s) q w"))
+        def load_rows(g):
+            for planes, scales in ((w1_planes, w1_scales), (w3_planes, w3_scales)):
+                load_plane(nc.sync, planes[g][:], scales[g * GROUP:(g + 1) * GROUP].rearrange("e s q w -> (e s) q w"))
 
         def load_w1(e):
             load_words(nc, w1_t[e], w1_words[e])
@@ -113,26 +106,37 @@ def tile_moe_ecr_glu_relu_kernel(
         def load_w3(e):
             load_words(nc, w3_t[e], w3_words[e])
 
+        slot_words = {}
+
+        def gather_words(e0, s, words):
+            window = x_t[s][:].bitcast(U32)
+            nc.vector.tensor_copy(words[:], window.indirect(entries(offs_t, e0 * C, (e0 + 2) * C)))
+            for j in range(2):
+                slot_words[e0 + j, s] = words[:, j * C:(j + 1) * C]
+
         load_tokens(0)
+        nc.sync.dma_start(offs_t[:], offs)
+        x_rows = x_scales.rearrange("s (q r) t -> r q s t", r=4)
+        for r in range(4):
+            nc.sync.dma_start(out=x_plane[r:P:16, 0:T].bitcast(I32), in_=x_rows[r].bitcast(I32))
         load_w1(0)
-        load_rows(w1_planes, w1_scales, W1_RUNS, 0)
+        load_w1(1)
+        load_rows(0)
         load_tokens(1)
-        for e in (1, 2, 3):
-            load_w1(e)
+        load_w3(0)
+        gather_words(0, 0, keep.tile([P, 2 * C], U32, name="words00", align_bytes=64))
         nc.vector.tensor_copy(slot_planes[0][:], x_plane[:].indirect(offs_t[:]))
         for r in range(4):
             nc.sync.dma_start(out=slot_planes[1][r:P:32, :].bitcast(I32), in_=slot_planes[0][16 + r:P:32, :].bitcast(I32))
-        load_w3(0)
-        load_rows(w3_planes, w3_scales, W3_RUNS, 0)
         load_w3(1)
+        load_w1(2)
         load_w3(2)
-        load_w1(4)
-        load_rows(w1_planes, w1_scales, W1_RUNS, 1)
-        load_w1(5)
+        load_w1(3)
+        load_rows(1)
         load_w3(3)
-        load_rows(w3_planes, w3_scales, W3_RUNS, 1)
-        load_w3(4)
-        load_w3(5)
+        for e in (4, 5):
+            load_w1(e)
+            load_w3(e)
         load_plane(nc.sync, w2_plane[:], w2_scales.rearrange("e s q w -> (e s) q w"))
         load_words(nc, w2_t, w2_words.rearrange("e s p b -> (e s) p b"))
 
@@ -149,13 +153,10 @@ def tile_moe_ecr_glu_relu_kernel(
 
         nc.scalar.activation(y[:, S:S + PAD], ident[:, 0:PAD], ACT.Relu, scale=-1.0)
 
-        slot_words = {}
-        for e0, s in ((0, 0), (2, 0), (0, 1), (2, 1), (4, 0), (4, 1)):
-            words = keep.tile([P, 2 * C], U32, name="words%d%d" % (e0, s), align_bytes=64)
-            window = x_t[s][:].bitcast(U32)
-            nc.vector.tensor_copy(words[:], window.indirect(entries(offs_t, e0 * C, (e0 + 2) * C)))
-            for j in range(2):
-                slot_words[e0 + j, s] = words[:, j * C:(j + 1) * C]
+        for j, e0 in enumerate((2, 4)):
+            gather_words(e0, 0, shared.tile([P, 2 * C], U32, name="words%d0" % e0, align_bytes=64, offset=j * BYTE_WINDOW))
+        for e0 in (0, 2, 4):
+            gather_words(e0, 1, keep.tile([P, 2 * C], U32, name="words%d1" % e0, align_bytes=64))
 
         def first_layer(dst, e, s, words, plane):
             nc.tensor.matmul_mx(
@@ -169,23 +170,22 @@ def tile_moe_ecr_glu_relu_kernel(
         hidden, quantised = {}, {}
 
         relu_a = {}
-        expert_bytes = PASSES * H
+
+        def plane_of(planes, e):
+            return planes[e // GROUP][:, (e % GROUP) * expert_bytes:(e % GROUP + 1) * expert_bytes]
 
         def gate_pass(e, s, dst):
-            run = 0 if e < W1_RUNS[0][1] else 1
-            j = e - W1_RUNS[run][0]
-            first_layer(dst, e, s, w1_t[e][:], w1_planes[run][:, j * expert_bytes:(j + 1) * expert_bytes])
+            first_layer(dst, e, s, w1_t[e][:], plane_of(w1_planes, e))
             if s == PASSES - 1:
                 relu_a[e] = keep.tile([P, 2, P, 2], F32, name="relu_a%d" % e, align_bytes=64)
                 nc.scalar.activation(relu_a[e][:], by_pair(dst[:]), ACT.Relu)
 
-        def value_branch(e, dst):
-            j = e % 3
-            for s in range(PASSES):
-                first_layer(dst, e, s, w3_t[e][:], w3_planes[e // 3][:, j * expert_bytes:(j + 1) * expert_bytes])
-            hidden[e] = keep.tile([P, 2, P, 2], BF16, name="h%d" % e, align_bytes=64)
-            for u0, u1 in ((0, 2),) if e < E - 1 else ((0, 1), (1, 2)):
-                nc.vector.tensor_tensor(hidden[e][:, u0:u1], by_pair(dst[:])[:, u0:u1], relu_a[e][:, u0:u1], ALU.mult)
+        def value_pass(e, s, dst):
+            first_layer(dst, e, s, w3_t[e][:], plane_of(w3_planes, e))
+            if s == PASSES - 1:
+                hidden[e] = keep.tile([P, 2, P, 2], BF16, name="h%d" % e, align_bytes=64)
+                for u0, u1 in ((0, 2),) if e < E - 1 else ((0, 1), (1, 2)):
+                    nc.vector.tensor_tensor(hidden[e][:, u0:u1], by_pair(dst[:])[:, u0:u1], relu_a[e][:, u0:u1], ALU.mult)
 
         def turn_and_quantise(e0, e1, room_bank):
             n = e1 - e0
@@ -217,29 +217,36 @@ def tile_moe_ecr_glu_relu_kernel(
                 )
             nc.scalar.copy(y[:, e0 * C:e1 * C], dst[:, 0:(e1 - e0) * C])
 
-        first_banks = [bank(b) for b in (0, 1, 6, 7)]
-        for s in range(PASSES):
-            for e in range(4):
-                gate_pass(e, s, first_banks[e])
-
         def gate_branch(e, dst):
             for s in range(PASSES):
                 gate_pass(e, s, dst)
 
-        for e in range(3):
-            value_branch(e, bank(2 + e))
-        gate_branch(4, bank(0))
-        turn_and_quantise(0, 2, 2)
-        gate_branch(5, bank(1))
-        turn_and_quantise(2, 3, 3)
-        value_branch(3, bank(5))
-        value_branch(4, bank(7))
-        value_branch(5, bank(6))
-        turn_and_quantise(3, 4, 0)
-        turn_and_quantise(4, 5, 1)
-        turn_and_quantise(5, 6, 4)
-        second_layer(0, 4, bank(6))
-        second_layer(4, 5, bank(2))
+        def value_branch(e, dst):
+            for s in range(PASSES):
+                value_pass(e, s, dst)
+
+        a0, a1, b0 = bank(0), bank(1), bank(2)
+        gate_pass(0, 0, a0)
+        gate_pass(1, 0, a1)
+        value_pass(0, 0, b0)
+        gate_pass(0, 1, a0)
+        value_pass(0, 1, b0)
+        gate_pass(1, 1, a1)
+        value_branch(1, bank(3))
+        gate_branch(2, bank(4))
+        value_branch(2, bank(5))
+        turn_and_quantise(0, 2, 0)
+        gate_branch(3, bank(6))
+        value_branch(3, bank(7))
+        gate_branch(4, bank(4))
+        value_branch(4, bank(1))
+        gate_branch(5, bank(2))
+        value_branch(5, bank(3))
+        turn_and_quantise(2, 3, 1)
+        turn_and_quantise(3, 5, 2)
+        turn_and_quantise(5, 6, 6)
+        second_layer(0, 3, bank(3))
+        second_layer(3, 5, bank(0))
         second_layer(5, 6, bank(5))
 
         product = [keep.tile([P, T], F32, name="product%d" % r) for r in range(TOP)]

@@ -13,8 +13,10 @@ PER_COL = 16
 FLOPS = 2 * S * (2 * K * H + H * N)
 BYTES = PASSES * T * (4 * P + 16) + E * (2 * PASSES * H + N) * (2 * P + 16) + 4 * TOP * T + 2 * P * (S + TOP * T) // PER_COL + 4 * N * T
 
-GROUP = 3
-BYTE_WINDOW = 1024
+W1_RUNS = ((0, 4), (4, 6))
+W3_RUNS = ((0, 3), (3, 6))
+PASS_PITCH = 1536
+WORD_TILE = 1024
 TURNED_TOKENS = 384
 
 F32 = mybir.dt.float32
@@ -66,28 +68,27 @@ def tile_moe_ecr_glu_relu_kernel(
             return psum.tile([P, 512], F32, name="bank", tag="bank%d" % b)
 
         shared = ctx.enter_context(tc.tile_pool(name="shared", bufs=1))
-        x_plane = shared.tile([P, BYTE_WINDOW], U8, name="x_plane", align_bytes=64, offset=BYTE_WINDOW // 2)
-        slot_planes = [keep.tile([P, S], U8, name="slot_plane%d" % s, align_bytes=64) for s in range(PASSES)]
+        x_plane = shared.tile([P, PASSES * PASS_PITCH], U8, name="x_plane", align_bytes=64, offset=WORD_TILE // 2)
+        x_live = x_plane[:].bitcast(I32).rearrange("p (s w) -> p s w", s=PASSES)[:, :, 0:T // 4]
         expert_bytes = PASSES * H
-        w1_planes = [keep.tile([P, GROUP * expert_bytes], U8, name="w1_plane%d" % g, align_bytes=64) for g in range(2)]
-        w3_planes = [keep.tile([P, GROUP * expert_bytes], U8, name="w3_plane%d" % g, align_bytes=64) for g in range(2)]
+        w1_planes = [keep.tile([P, (e1 - e0) * expert_bytes], U8, name="w1_plane%d" % e0, align_bytes=64)
+                     for e0, e1 in W1_RUNS]
+        w3_planes = [keep.tile([P, (e1 - e0) * expert_bytes], U8, name="w3_plane%d" % e0, align_bytes=64)
+                     for e0, e1 in W3_RUNS]
         w2_plane = keep.tile([P, E * N], U8, name="w2_plane", align_bytes=64)
         y = keep.tile([P, S + PAD], F32, name="y", align_bytes=64)
         ident = keep.tile([P, P], F32, name="ident")
-        nc.gpsimd.memset(x_plane[:, 0:T].bitcast(I32), 0)
+        nc.gpsimd.memset(x_live, 0)
         nc.gpsimd.memset(w1_planes[0][:].bitcast(I32), 0)
         nc.vector.memset(w3_planes[0][:].bitcast(I32), 0)
-        nc.vector.memset(w1_planes[1][:].bitcast(I32), 0)
-        nc.gpsimd.memset(x_plane[:, T:].bitcast(I32), 0)
+        nc.vector.memset(w3_planes[1][:].bitcast(I32), 0)
         make_identity(nc, ident[:])
-        nc.gpsimd.memset(slot_planes[1][:].bitcast(I32), 0)
-        nc.gpsimd.memset(w3_planes[1][:].bitcast(I32), 0)
+        nc.gpsimd.memset(w1_planes[1][:].bitcast(I32), 0)
         nc.gpsimd.memset(w2_plane[:].bitcast(I32), 0)
 
         offs_t = keep.tile([P, S // PER_COL], U16, name="offs_t")
         x_t = [keep.tile([P, T], I32, name="x_t%d" % s, align_bytes=64) for s in range(PASSES)]
-        w1_t = [keep.tile([P, PASSES * 2 * H], U8, name="w1_t%d" % e, align_bytes=64) for e in range(E)]
-        w3_t = [keep.tile([P, PASSES * 2 * H], U8, name="w3_t%d" % e, align_bytes=64) for e in range(E)]
+        w1_t, w3_t = {}, {}
         w2_t = keep.tile([P, E * 2 * N], U8, name="w2_t", align_bytes=64)
         pos_t = [keep.tile([P, T // PER_COL], U16, name="pos_t%d" % r) for r in range(TOP)]
         token_parts = ((0, TURNED_TOKENS), (TURNED_TOKENS, T))
@@ -96,47 +97,40 @@ def tile_moe_ecr_glu_relu_kernel(
         def load_tokens(s):
             nc.sync.dma_start(out=x_t[s][:], in_=x_words[s].rearrange("p t r -> p (t r)").bitcast(I32))
 
-        def load_rows(g):
-            for planes, scales in ((w1_planes, w1_scales), (w3_planes, w3_scales)):
-                load_plane(nc.sync, planes[g][:], scales[g * GROUP:(g + 1) * GROUP].rearrange("e s q w -> (e s) q w"))
+        def load_rows(planes, scales, runs, run):
+            e0, e1 = runs[run]
+            load_plane(nc.sync, planes[run][:], scales[e0:e1].rearrange("e s q w -> (e s) q w"))
 
-        def load_w1(e):
-            load_words(nc, w1_t[e], w1_words[e])
+        def load_experts(found, words, name, e0, e1):
+            tile = keep.tile([P, (e1 - e0) * 2 * expert_bytes], U8, name="%s_t%d" % (name, e0), align_bytes=64)
+            load_words(nc, tile, words[e0:e1].rearrange("e s p b -> (e s) p b"))
+            for e in range(e0, e1):
+                found[e] = tile[:, (e - e0) * 2 * expert_bytes:(e - e0 + 1) * 2 * expert_bytes]
 
-        def load_w3(e):
-            load_words(nc, w3_t[e], w3_words[e])
+        def load_w1(e0, e1):
+            load_experts(w1_t, w1_words, "w1", e0, e1)
 
-        slot_words = {}
-
-        def gather_words(e0, s, words):
-            window = x_t[s][:].bitcast(U32)
-            nc.vector.tensor_copy(words[:], window.indirect(entries(offs_t, e0 * C, (e0 + 2) * C)))
-            for j in range(2):
-                slot_words[e0 + j, s] = words[:, j * C:(j + 1) * C]
+        def load_w3(e0, e1):
+            load_experts(w3_t, w3_words, "w3", e0, e1)
 
         load_tokens(0)
         nc.sync.dma_start(offs_t[:], offs)
+        load_tokens(1)
         x_rows = x_scales.rearrange("s (q r) t -> r q s t", r=4)
         for r in range(4):
-            nc.sync.dma_start(out=x_plane[r:P:16, 0:T].bitcast(I32), in_=x_rows[r].bitcast(I32))
-        load_w1(0)
-        load_w1(1)
-        load_rows(0)
-        load_tokens(1)
-        load_w3(0)
-        gather_words(0, 0, keep.tile([P, 2 * C], U32, name="words00", align_bytes=64))
-        nc.vector.tensor_copy(slot_planes[0][:], x_plane[:].indirect(offs_t[:]))
-        for r in range(4):
-            nc.sync.dma_start(out=slot_planes[1][r:P:32, :].bitcast(I32), in_=slot_planes[0][16 + r:P:32, :].bitcast(I32))
-        load_w3(1)
-        load_w1(2)
-        load_w3(2)
-        load_w1(3)
-        load_rows(1)
-        load_w3(3)
-        for e in (4, 5):
-            load_w1(e)
-            load_w3(e)
+            nc.sync.dma_start(out=x_live[r:P:32], in_=x_rows[r].bitcast(I32))
+        load_w1(0, 2)
+        load_rows(w1_planes, w1_scales, W1_RUNS, 0)
+        load_w3(0, 2)
+        load_rows(w3_planes, w3_scales, W3_RUNS, 0)
+        load_w1(2, 4)
+        load_w3(2, 3)
+        load_rows(w1_planes, w1_scales, W1_RUNS, 1)
+        load_w1(4, 6)
+        load_w3(3, 4)
+        load_rows(w3_planes, w3_scales, W3_RUNS, 1)
+        load_w3(4, 5)
+        load_w3(5, 6)
         load_plane(nc.sync, w2_plane[:], w2_scales.rearrange("e s q w -> (e s) q w"))
         load_words(nc, w2_t, w2_words.rearrange("e s p b -> (e s) p b"))
 
@@ -153,15 +147,30 @@ def tile_moe_ecr_glu_relu_kernel(
 
         nc.scalar.activation(y[:, S:S + PAD], ident[:, 0:PAD], ACT.Relu, scale=-1.0)
 
-        for j, e0 in enumerate((2, 4)):
-            gather_words(e0, 0, shared.tile([P, 2 * C], U32, name="words%d0" % e0, align_bytes=64, offset=j * BYTE_WINDOW))
+        slot_words, slot_planes = {}, {}
+
+        def gather(found, e0, s, window, dst):
+            nc.vector.tensor_copy(dst[:], window.indirect(entries(offs_t, e0 * C, (e0 + 2) * C)))
+            for j in range(2):
+                found[e0 + j, s] = dst[:, j * C:(j + 1) * C]
+
+        for s in range(PASSES):
+            dst = keep.tile([P, 2 * C], U32, name="words0%d" % s, align_bytes=64)
+            gather(slot_words, 0, s, x_t[s][:].bitcast(U32), dst)
         for e0 in (0, 2, 4):
-            gather_words(e0, 1, keep.tile([P, 2 * C], U32, name="words%d1" % e0, align_bytes=64))
+            for s in range(PASSES):
+                dst = keep.tile([P, 2 * C], U8, name="bytes%d%d" % (e0, s), align_bytes=64)
+                gather(slot_planes, e0, s, x_plane[:, s * PASS_PITCH:s * PASS_PITCH + T], dst)
+        for e0 in (2, 4):
+            for s in range(PASSES):
+                dst = shared.tile([P, 2 * C], U32, name="words%d%d" % (e0, s), align_bytes=64,
+                                  offset=(e0 - 2 + s) * WORD_TILE)
+                gather(slot_words, e0, s, x_t[s][:].bitcast(U32), dst)
 
         def first_layer(dst, e, s, words, plane):
             nc.tensor.matmul_mx(
                 out=dst[:],
-                lhsT=slot_words[e, s].bitcast(FP8X4), lhsT_scale=slot_planes[s][:, e * C:(e + 1) * C],
+                lhsT=slot_words[e, s].bitcast(FP8X4), lhsT_scale=slot_planes[e, s],
                 rhs=words[:, 2 * s * H:2 * (s + 1) * H].bitcast(FP4X4),
                 rhs_scale=plane[:, s * H:(s + 1) * H],
                 start=(s == 0), stop=(s == PASSES - 1),
@@ -171,17 +180,19 @@ def tile_moe_ecr_glu_relu_kernel(
 
         relu_a = {}
 
-        def plane_of(planes, e):
-            return planes[e // GROUP][:, (e % GROUP) * expert_bytes:(e % GROUP + 1) * expert_bytes]
+        def plane_of(planes, runs, e):
+            run = 0 if e < runs[0][1] else 1
+            j = e - runs[run][0]
+            return planes[run][:, j * expert_bytes:(j + 1) * expert_bytes]
 
         def gate_pass(e, s, dst):
-            first_layer(dst, e, s, w1_t[e][:], plane_of(w1_planes, e))
+            first_layer(dst, e, s, w1_t[e], plane_of(w1_planes, W1_RUNS, e))
             if s == PASSES - 1:
                 relu_a[e] = keep.tile([P, 2, P, 2], F32, name="relu_a%d" % e, align_bytes=64)
                 nc.scalar.activation(relu_a[e][:], by_pair(dst[:]), ACT.Relu)
 
         def value_pass(e, s, dst):
-            first_layer(dst, e, s, w3_t[e][:], plane_of(w3_planes, e))
+            first_layer(dst, e, s, w3_t[e], plane_of(w3_planes, W3_RUNS, e))
             if s == PASSES - 1:
                 hidden[e] = keep.tile([P, 2, P, 2], BF16, name="h%d" % e, align_bytes=64)
                 for u0, u1 in ((0, 2),) if e < E - 1 else ((0, 1), (1, 2)):
@@ -225,29 +236,25 @@ def tile_moe_ecr_glu_relu_kernel(
             for s in range(PASSES):
                 value_pass(e, s, dst)
 
-        a0, a1, b0 = bank(0), bank(1), bank(2)
-        gate_pass(0, 0, a0)
-        gate_pass(1, 0, a1)
-        value_pass(0, 0, b0)
-        gate_pass(0, 1, a0)
-        value_pass(0, 1, b0)
-        gate_pass(1, 1, a1)
+        gate_branch(0, bank(0))
+        gate_branch(1, bank(1))
+        value_branch(0, bank(2))
         value_branch(1, bank(3))
-        gate_branch(2, bank(4))
+        gate_branch(2, bank(6))
+        gate_branch(3, bank(7))
         value_branch(2, bank(5))
-        turn_and_quantise(0, 2, 0)
-        gate_branch(3, bank(6))
-        value_branch(3, bank(7))
-        gate_branch(4, bank(4))
-        value_branch(4, bank(1))
-        gate_branch(5, bank(2))
-        value_branch(5, bank(3))
-        turn_and_quantise(2, 3, 1)
-        turn_and_quantise(3, 5, 2)
-        turn_and_quantise(5, 6, 6)
-        second_layer(0, 3, bank(3))
-        second_layer(3, 5, bank(0))
-        second_layer(5, 6, bank(5))
+        turn_and_quantise(0, 2, 7)
+        turn_and_quantise(2, 3, 0)
+        gate_branch(4, bank(6))
+        gate_branch(5, bank(1))
+        for e, b in ((3, 2), (4, 3), (5, 4)):
+            value_branch(e, bank(b))
+        turn_and_quantise(3, 4, 7)
+        turn_and_quantise(4, 5, 5)
+        turn_and_quantise(5, 6, 0)
+        second_layer(0, 3, bank(4))
+        second_layer(3, 5, bank(6))
+        second_layer(5, 6, bank(1))
 
         product = [keep.tile([P, T], F32, name="product%d" % r) for r in range(TOP)]
         result = keep.tile([P, T], F32, name="result")

@@ -79,12 +79,9 @@ def tile_moe_ecr_glu_relu_kernel(
         y = keep.tile([P, S + PAD], F32, name="y", align_bytes=64)
         ident = keep.tile([P, P], F32, name="ident")
         nc.gpsimd.memset(x_live, 0)
-        nc.gpsimd.memset(w1_planes[0][:].bitcast(I32), 0)
-        nc.vector.memset(w3_planes[0][:].bitcast(I32), 0)
-        nc.vector.memset(w3_planes[1][:].bitcast(I32), 0)
         make_identity(nc, ident[:])
-        nc.gpsimd.memset(w1_planes[1][:].bitcast(I32), 0)
-        nc.gpsimd.memset(w2_plane[:].bitcast(I32), 0)
+        for plane in (w1_planes[0], w3_planes[0], w1_planes[1], w3_planes[1], w2_plane):
+            nc.vector.memset(plane[:].bitcast(I32), 0)
 
         offs_t = keep.tile([P, S // PER_COL], U16, name="offs_t")
         x_t = [keep.tile([P, T], I32, name="x_t%d" % s, align_bytes=64) for s in range(PASSES)]

@@ -158,11 +158,14 @@ def tile_moe_ecr_glu_relu_kernel(
             for s in range(PASSES):
                 dst = keep.tile([P, 2 * C], U8, name="bytes%d%d" % (e0, s), align_bytes=64)
                 gather(slot_planes, e0, s, x_plane[:, s * PASS_PITCH:s * PASS_PITCH + T], dst)
-        for e0 in (2, 4):
+
+        def gather_late_words(e0, first_tile):
             for s in range(PASSES):
                 dst = shared.tile([P, 2 * C], U32, name="words%d%d" % (e0, s), align_bytes=64,
-                                  offset=(e0 - 2 + s) * WORD_TILE)
+                                  offset=(first_tile + s) * WORD_TILE)
                 gather(slot_words, e0, s, x_t[s][:].bitcast(U32), dst)
+
+        gather_late_words(2, 0)
 
         def first_layer(dst, e, s, words, plane):
             nc.tensor.matmul_mx(
@@ -185,7 +188,10 @@ def tile_moe_ecr_glu_relu_kernel(
         def gate_pass(e, s, dst):
             first_layer(dst, e, s, w1_t[e], plane_of(w1_planes, W1_RUNS, e))
             if s == PASSES - 1:
-                relu_a[e] = keep.tile([P, 2, P, 2], F32, name="relu_a%d" % e, align_bytes=64)
+                if e == 1:
+                    relu_a[e] = shared.tile([P, 2, P, 2], F32, name="relu_a1", align_bytes=64, offset=4 * WORD_TILE)
+                else:
+                    relu_a[e] = keep.tile([P, 2, P, 2], F32, name="relu_a%d" % e, align_bytes=64)
                 nc.scalar.activation(relu_a[e][:], by_pair(dst[:]), ACT.Relu)
 
         def value_pass(e, s, dst):
@@ -237,15 +243,16 @@ def tile_moe_ecr_glu_relu_kernel(
         gate_branch(1, bank(1))
         value_branch(0, bank(2))
         value_branch(1, bank(3))
+        gather_late_words(4, 4)
         gate_branch(2, bank(6))
         gate_branch(3, bank(7))
         value_branch(2, bank(5))
         turn_and_quantise(0, 2, 7)
-        turn_and_quantise(2, 3, 0)
         gate_branch(4, bank(6))
         gate_branch(5, bank(1))
         for e, b in ((3, 2), (4, 3), (5, 4)):
             value_branch(e, bank(b))
+        turn_and_quantise(2, 3, 2)
         turn_and_quantise(3, 4, 7)
         turn_and_quantise(4, 5, 5)
         turn_and_quantise(5, 6, 0)

@@ -118,16 +118,15 @@ def tile_moe_ecr_glu_relu_kernel(
             nc.sync.dma_start(out=x_live[r:P:32], in_=x_rows[r].bitcast(I32))
         load_w1(0, 2)
         load_rows(w1_planes, w1_scales, W1_RUNS, 0)
-        load_w3(0, 2)
         load_rows(w3_planes, w3_scales, W3_RUNS, 0)
+        load_w3(0, 2)
         load_w1(2, 4)
         load_w3(2, 3)
-        load_rows(w1_planes, w1_scales, W1_RUNS, 1)
         load_w1(4, 6)
-        load_w3(3, 4)
+        load_rows(w1_planes, w1_scales, W1_RUNS, 1)
         load_rows(w3_planes, w3_scales, W3_RUNS, 1)
-        load_w3(4, 5)
-        load_w3(5, 6)
+        for e in range(3, E):
+            load_w3(e, e + 1)
         load_plane(nc.sync, w2_plane[:], w2_scales.rearrange("e s q w -> (e s) q w"))
         load_words(nc, w2_t, w2_words.rearrange("e s p b -> (e s) p b"))
 

@@ -80,8 +80,6 @@ def tile_moe_ecr_glu_relu_kernel(
         ident = keep.tile([P, P], F32, name="ident")
         nc.gpsimd.memset(x_live, 0)
         make_identity(nc, ident[:])
-        for plane in (w1_planes[0], w3_planes[0], w1_planes[1], w3_planes[1], w2_plane):
-            nc.vector.memset(plane[:].bitcast(I32), 0)
 
         offs_t = keep.tile([P, S // PER_COL], U16, name="offs_t")
         x_t = [keep.tile([P, T], I32, name="x_t%d" % s, align_bytes=64) for s in range(PASSES)]

@@ -13,7 +13,7 @@ PER_COL = 16
 FLOPS = 2 * S * (2 * K * H + H * N)
 BYTES = PASSES * T * (4 * P + 16) + E * (2 * PASSES * H + N) * (2 * P + 16) + 4 * TOP * T + 2 * P * (S + TOP * T) // PER_COL + 4 * N * T
 
-W1_RUNS = ((0, 4), (4, 6))
+W1_RUNS = ((0, 3), (3, 6))
 W3_RUNS = ((0, 3), (3, 6))
 PASS_PITCH = 1536
 WORD_TILE = 1024
@@ -118,12 +118,14 @@ def tile_moe_ecr_glu_relu_kernel(
         load_rows(w1_planes, w1_scales, W1_RUNS, 0)
         load_rows(w3_planes, w3_scales, W3_RUNS, 0)
         load_w3(0, 2)
-        load_w1(2, 4)
+        load_w1(2, 3)
         load_w3(2, 3)
-        load_w1(4, 6)
+        load_w1(3, 4)
         load_rows(w1_planes, w1_scales, W1_RUNS, 1)
         load_rows(w3_planes, w3_scales, W3_RUNS, 1)
-        for e in range(3, E):
+        load_w3(3, 4)
+        for e in range(4, E):
+            load_w1(e, e + 1)
             load_w3(e, e + 1)
         load_plane(nc.sync, w2_plane[:], w2_scales.rearrange("e s q w -> (e s) q w"))
         load_words(nc, w2_t, w2_words.rearrange("e s p b -> (e s) p b"))
@@ -182,6 +184,9 @@ def tile_moe_ecr_glu_relu_kernel(
             j = e - runs[run][0]
             return planes[run][:, j * expert_bytes:(j + 1) * expert_bytes]
 
+        def halves(e):
+            return ((0, 2),) if e < E - 1 else ((0, 1), (1, 2))
+
         def gate_pass(e, s, dst):
             first_layer(dst, e, s, w1_t[e], plane_of(w1_planes, W1_RUNS, e))
             if s == PASSES - 1:
@@ -189,13 +194,14 @@ def tile_moe_ecr_glu_relu_kernel(
                     relu_a[e] = shared.tile([P, 2, P, 2], F32, name="relu_a1", align_bytes=64, offset=4 * WORD_TILE)
                 else:
                     relu_a[e] = keep.tile([P, 2, P, 2], F32, name="relu_a%d" % e, align_bytes=64)
-                nc.scalar.activation(relu_a[e][:], by_pair(dst[:]), ACT.Relu)
+                for u0, u1 in halves(e):
+                    nc.scalar.activation(relu_a[e][:, u0:u1], by_pair(dst[:])[:, u0:u1], ACT.Relu)
 
         def value_pass(e, s, dst):
             first_layer(dst, e, s, w3_t[e], plane_of(w3_planes, W3_RUNS, e))
             if s == PASSES - 1:
                 hidden[e] = keep.tile([P, 2, P, 2], BF16, name="h%d" % e, align_bytes=64)
-                for u0, u1 in ((0, 2),) if e < E - 1 else ((0, 1), (1, 2)):
+                for u0, u1 in halves(e):
                     nc.vector.tensor_tensor(hidden[e][:, u0:u1], by_pair(dst[:])[:, u0:u1], relu_a[e][:, u0:u1], ALU.mult)
 
         def turn_and_quantise(e0, e1, room_bank):
@@ -242,20 +248,18 @@ def tile_moe_ecr_glu_relu_kernel(
         value_branch(1, bank(3))
         gather_late_words(4, 4)
         gate_branch(2, bank(6))
-        gate_branch(3, bank(7))
         value_branch(2, bank(5))
-        turn_and_quantise(0, 2, 7)
-        gate_branch(4, bank(6))
-        gate_branch(5, bank(1))
-        for e, b in ((3, 2), (4, 3), (5, 4)):
-            value_branch(e, bank(b))
-        turn_and_quantise(2, 3, 2)
-        turn_and_quantise(3, 4, 7)
-        turn_and_quantise(4, 5, 5)
-        turn_and_quantise(5, 6, 0)
+        turn_and_quantise(0, 2, 6)
+        for e, a_bank, b_bank in ((3, 7, 2), (4, 0, 3), (5, 1, 4)):
+            gate_branch(e, bank(a_bank))
+            value_branch(e, bank(b_bank))
+        turn_and_quantise(2, 3, 3)
+        turn_and_quantise(3, 4, 1)
+        turn_and_quantise(4, 5, 0)
+        turn_and_quantise(5, 6, 2)
         second_layer(0, 3, bank(4))
         second_layer(3, 5, bank(6))
-        second_layer(5, 6, bank(1))
+        second_layer(5, 6, bank(7))
 
         product = [keep.tile([P, T], F32, name="product%d" % r) for r in range(TOP)]
         result = keep.tile([P, T], F32, name="result")

@@ -19,6 +19,8 @@ PASS_PITCH = 1536
 WORD_TILE = 1024
 TURNED_TOKENS = 384
 
+ALIGN = 256
+
 F32 = mybir.dt.float32
 BF16 = mybir.dt.bfloat16
 I32 = mybir.dt.int32
@@ -68,26 +70,26 @@ def tile_moe_ecr_glu_relu_kernel(
             return psum.tile([P, 512], F32, name="bank", tag="bank%d" % b)
 
         shared = ctx.enter_context(tc.tile_pool(name="shared", bufs=1))
-        x_plane = shared.tile([P, PASSES * PASS_PITCH], U8, name="x_plane", align_bytes=64, offset=WORD_TILE // 2)
+        x_plane = shared.tile([P, PASSES * PASS_PITCH], U8, name="x_plane", align_bytes=ALIGN, offset=WORD_TILE // 2)
         x_live = x_plane[:].bitcast(I32).rearrange("p (s w) -> p s w", s=PASSES)[:, :, 0:T // 4]
         expert_bytes = PASSES * H
-        w1_planes = [keep.tile([P, (e1 - e0) * expert_bytes], U8, name="w1_plane%d" % e0, align_bytes=64)
+        w1_planes = [keep.tile([P, (e1 - e0) * expert_bytes], U8, name="w1_plane%d" % e0, align_bytes=ALIGN)
                      for e0, e1 in W1_RUNS]
-        w3_planes = [keep.tile([P, (e1 - e0) * expert_bytes], U8, name="w3_plane%d" % e0, align_bytes=64)
+        w3_planes = [keep.tile([P, (e1 - e0) * expert_bytes], U8, name="w3_plane%d" % e0, align_bytes=ALIGN)
                      for e0, e1 in W3_RUNS]
-        w2_plane = keep.tile([P, E * N], U8, name="w2_plane", align_bytes=64)
-        y = keep.tile([P, S + PAD], F32, name="y", align_bytes=64)
-        ident = keep.tile([P, P], F32, name="ident")
+        w2_plane = keep.tile([P, E * N], U8, name="w2_plane", align_bytes=ALIGN)
+        y = keep.tile([P, S + PAD], F32, name="y", align_bytes=ALIGN)
+        ident = keep.tile([P, P], F32, name="ident", align_bytes=ALIGN)
         nc.gpsimd.memset(x_live, 0)
         make_identity(nc, ident[:])
 
         offs_t = keep.tile([P, S // PER_COL], U16, name="offs_t")
-        x_t = [keep.tile([P, T], I32, name="x_t%d" % s, align_bytes=64) for s in range(PASSES)]
+        x_t = [keep.tile([P, T], I32, name="x_t%d" % s, align_bytes=ALIGN) for s in range(PASSES)]
         w1_t, w3_t = {}, {}
-        w2_t = keep.tile([P, E * 2 * N], U8, name="w2_t", align_bytes=64)
+        w2_t = keep.tile([P, E * 2 * N], U8, name="w2_t", align_bytes=ALIGN)
         pos_t = [keep.tile([P, T // PER_COL], U16, name="pos_t%d" % r) for r in range(TOP)]
         token_parts = ((0, TURNED_TOKENS), (TURNED_TOKENS, T))
-        gate_t = {t0: keep.tile([P, TOP * (t1 - t0)], F32, name="gate_t%d" % t0) for t0, t1 in token_parts}
+        gate_t = {t0: keep.tile([P, TOP * (t1 - t0)], F32, name="gate_t%d" % t0, align_bytes=ALIGN) for t0, t1 in token_parts}
 
         def load_tokens(s):
             nc.sync.dma_start(out=x_t[s][:], in_=x_words[s].rearrange("p t r -> p (t r)").bitcast(I32))
@@ -97,7 +99,7 @@ def tile_moe_ecr_glu_relu_kernel(
             load_plane(nc.sync, planes[run][:], scales[e0:e1].rearrange("e s q w -> (e s) q w"))
 
         def load_experts(found, words, name, e0, e1):
-            tile = keep.tile([P, (e1 - e0) * 2 * expert_bytes], U8, name="%s_t%d" % (name, e0), align_bytes=64)
+            tile = keep.tile([P, (e1 - e0) * 2 * expert_bytes], U8, name="%s_t%d" % (name, e0), align_bytes=ALIGN)
             load_words(nc, tile, words[e0:e1].rearrange("e s p b -> (e s) p b"))
             for e in range(e0, e1):
                 found[e] = tile[:, (e - e0) * 2 * expert_bytes:(e - e0 + 1) * 2 * expert_bytes]
@@ -151,16 +153,16 @@ def tile_moe_ecr_glu_relu_kernel(
                 found[e0 + j, s] = dst[:, j * C:(j + 1) * C]
 
         for s in range(PASSES):
-            dst = keep.tile([P, 2 * C], U32, name="words0%d" % s, align_bytes=64)
+            dst = keep.tile([P, 2 * C], U32, name="words0%d" % s, align_bytes=ALIGN)
             gather(slot_words, 0, s, x_t[s][:].bitcast(U32), dst)
         for e0 in (0, 2, 4):
             for s in range(PASSES):
-                dst = keep.tile([P, 2 * C], U8, name="bytes%d%d" % (e0, s), align_bytes=64)
+                dst = keep.tile([P, 2 * C], U8, name="bytes%d%d" % (e0, s), align_bytes=ALIGN)
                 gather(slot_planes, e0, s, x_plane[:, s * PASS_PITCH:s * PASS_PITCH + T], dst)
 
         def gather_late_words(e0, first_tile):
             for s in range(PASSES):
-                dst = shared.tile([P, 2 * C], U32, name="words%d%d" % (e0, s), align_bytes=64,
+                dst = shared.tile([P, 2 * C], U32, name="words%d%d" % (e0, s), align_bytes=ALIGN,
                                   offset=(first_tile + s) * WORD_TILE)
                 gather(slot_words, e0, s, x_t[s][:].bitcast(U32), dst)
 
@@ -191,16 +193,16 @@ def tile_moe_ecr_glu_relu_kernel(
             first_layer(dst, e, s, w1_t[e], plane_of(w1_planes, W1_RUNS, e))
             if s == PASSES - 1:
                 if e == 1:
-                    relu_a[e] = shared.tile([P, 2, P, 2], F32, name="relu_a1", align_bytes=64, offset=4 * WORD_TILE)
+                    relu_a[e] = shared.tile([P, 2, P, 2], F32, name="relu_a1", align_bytes=ALIGN, offset=4 * WORD_TILE)
                 else:
-                    relu_a[e] = keep.tile([P, 2, P, 2], F32, name="relu_a%d" % e, align_bytes=64)
+                    relu_a[e] = keep.tile([P, 2, P, 2], F32, name="relu_a%d" % e, align_bytes=ALIGN)
                 for u0, u1 in halves(e):
                     nc.scalar.activation(relu_a[e][:, u0:u1], by_pair(dst[:])[:, u0:u1], ACT.Relu)
 
         def value_pass(e, s, dst):
             first_layer(dst, e, s, w3_t[e], plane_of(w3_planes, W3_RUNS, e))
             if s == PASSES - 1:
-                hidden[e] = keep.tile([P, 2, P, 2], BF16, name="h%d" % e, align_bytes=64)
+                hidden[e] = keep.tile([P, 2, P, 2], BF16, name="h%d" % e, align_bytes=ALIGN)
                 for u0, u1 in halves(e):
                     nc.vector.tensor_tensor(hidden[e][:, u0:u1], by_pair(dst[:])[:, u0:u1], relu_a[e][:, u0:u1], ALU.mult)
 
@@ -212,10 +214,10 @@ def tile_moe_ecr_glu_relu_kernel(
                 for u in range(2):
                     col = ((e - e0) * 2 + u) * P
                     nc.tensor.transpose(room[:, col:col + P], pairs[:, u * P:(u + 1) * P], ident[:])
-            turned = keep.tile([P, n, C, 2], F32, name="turned%d" % e0, align_bytes=64)
+            turned = keep.tile([P, n, C, 2], F32, name="turned%d" % e0, align_bytes=ALIGN)
             nc.scalar.copy(turned[:], room.rearrange("p (e u c) -> p e c u", e=n, u=2))
-            h_words = keep.tile([P, n * C], U32, name="h_words%d" % e0, align_bytes=64)
-            h_plane = keep.tile([P, n * C], U8, name="h_plane%d" % e0, align_bytes=64)
+            h_words = keep.tile([P, n * C], U32, name="h_words%d" % e0, align_bytes=ALIGN)
+            h_plane = keep.tile([P, n * C], U8, name="h_plane%d" % e0, align_bytes=ALIGN)
             nc.vector.quantize_mx(
                 out=h_words[:].bitcast(FP8X4), scales=h_plane[:],
                 in_=turned[:].rearrange("p e c u -> p (e c u)").bitcast(BF16),
@@ -261,8 +263,8 @@ def tile_moe_ecr_glu_relu_kernel(
         second_layer(3, 5, bank(6))
         second_layer(5, 6, bank(7))
 
-        product = [keep.tile([P, T], F32, name="product%d" % r) for r in range(TOP)]
-        result = keep.tile([P, T], F32, name="result")
+        product = [keep.tile([P, T], F32, name="product%d" % r, align_bytes=ALIGN) for r in range(TOP)]
+        result = keep.tile([P, T], F32, name="result", align_bytes=ALIGN)
 
         def fetch(r, t0, t1):
             nc.vector.tensor_tensor(product[r][:, t0:t1], y[:].indirect(entries(pos_t[r], t0, t1)),
@@ -277,14 +279,14 @@ def tile_moe_ecr_glu_relu_kernel(
                                  is_transpose=True, start=(r == 0), stop=(r == TOP - 1))
         back = bank(chunks)
         for c in range(chunks):
-            by_token = keep.tile([P, P], F32, name="by_token%d" % c)
+            by_token = keep.tile([P, P], F32, name="by_token%d" % c, align_bytes=ALIGN)
             nc.scalar.copy(by_token[:], sums[c][:, 0:P])
             nc.tensor.transpose(back[:, c * P:(c + 1) * P], by_token[:], ident[:])
         nc.scalar.copy(result[:, 0:TURNED_TOKENS], back[:, 0:TURNED_TOKENS])
         nc.scalar.dma_start(out=out[:, 0:TURNED_TOKENS], in_=result[:, 0:TURNED_TOKENS])
 
         rest = slice(TURNED_TOKENS, T)
-        partial = [keep.tile([P, T], F32, name="partial%d" % j) for j in range(TOP - 2)]
+        partial = [keep.tile([P, T], F32, name="partial%d" % j, align_bytes=ALIGN) for j in range(TOP - 2)]
         for r in range(TOP - 1):
             fetch(r, TURNED_TOKENS, T)
         nc.vector.tensor_tensor(partial[0][:, rest], product[0][:, rest], product[1][:, rest], ALU.add)

@@ -168,12 +168,12 @@ def tile_moe_ecr_glu_relu_kernel(
 
         gather_late_words(2, 0)
 
-        def first_layer(dst, e, s, words, plane):
+        def first_layer(dst, e, s, words, plane, i0=0, i1=H):
             nc.tensor.matmul_mx(
-                out=dst[:],
+                out=dst[:, 0:i1 - i0],
                 lhsT=slot_words[e, s].bitcast(FP8X4), lhsT_scale=slot_planes[e, s],
-                rhs=words[:, 2 * s * H:2 * (s + 1) * H].bitcast(FP4X4),
-                rhs_scale=plane[:, s * H:(s + 1) * H],
+                rhs=words[:, 2 * (s * H + i0):2 * (s * H + i1)].bitcast(FP4X4),
+                rhs_scale=plane[:, s * H + i0:s * H + i1],
                 start=(s == 0), stop=(s == PASSES - 1),
             )
 
@@ -187,7 +187,7 @@ def tile_moe_ecr_glu_relu_kernel(
             return planes[run][:, j * expert_bytes:(j + 1) * expert_bytes]
 
         def halves(e):
-            return ((0, 2),) if e < E - 1 else ((0, 1), (1, 2))
+            return ((0, P),) if e < E - 1 else ((0, P // 2), (P // 2, P))
 
         def gate_pass(e, s, dst):
             first_layer(dst, e, s, w1_t[e], plane_of(w1_planes, W1_RUNS, e))
@@ -196,17 +196,10 @@ def tile_moe_ecr_glu_relu_kernel(
                     relu_a[e] = shared.tile([P, 2, P, 2], F32, name="relu_a1", align_bytes=ALIGN, offset=4 * WORD_TILE)
                 else:
                     relu_a[e] = keep.tile([P, 2, P, 2], F32, name="relu_a%d" % e, align_bytes=ALIGN)
-                for u0, u1 in halves(e):
-                    nc.scalar.activation(relu_a[e][:, u0:u1], by_pair(dst[:])[:, u0:u1], ACT.Relu)
+                for p0, p1 in halves(e):
+                    nc.scalar.activation(relu_a[e][:, :, p0:p1], by_pair(dst[:])[:, :, p0:p1], ACT.Relu)
 
-        def value_pass(e, s, dst):
-            first_layer(dst, e, s, w3_t[e], plane_of(w3_planes, W3_RUNS, e))
-            if s == PASSES - 1:
-                hidden[e] = keep.tile([P, 2, P, 2], BF16, name="h%d" % e, align_bytes=ALIGN)
-                for u0, u1 in halves(e):
-                    nc.vector.tensor_tensor(hidden[e][:, u0:u1], by_pair(dst[:])[:, u0:u1], relu_a[e][:, u0:u1], ALU.mult)
-
-        def turn_and_quantise(e0, e1, room_bank):
+        def turn_and_quantise(e0, e1, room_bank, copy):
             n = e1 - e0
             room = bank(room_bank)[:, 0:n * 2 * P]
             for e in range(e0, e1):
@@ -215,7 +208,7 @@ def tile_moe_ecr_glu_relu_kernel(
                     col = ((e - e0) * 2 + u) * P
                     nc.tensor.transpose(room[:, col:col + P], pairs[:, u * P:(u + 1) * P], ident[:])
             turned = keep.tile([P, n, C, 2], F32, name="turned%d" % e0, align_bytes=ALIGN)
-            nc.scalar.copy(turned[:], room.rearrange("p (e u c) -> p e c u", e=n, u=2))
+            copy(turned[:], room.rearrange("p (e u c) -> p e c u", e=n, u=2))
             h_words = keep.tile([P, n * C], U32, name="h_words%d" % e0, align_bytes=ALIGN)
             h_plane = keep.tile([P, n * C], U8, name="h_plane%d" % e0, align_bytes=ALIGN)
             nc.vector.quantize_mx(
@@ -225,7 +218,7 @@ def tile_moe_ecr_glu_relu_kernel(
             for j in range(n):
                 quantised[e0 + j] = (h_words[:, j * C:(j + 1) * C], h_plane[:, j * C:(j + 1) * C])
 
-        def second_layer(e0, e1, dst):
+        def second_layer(e0, e1, dst, copy):
             for e in range(e0, e1):
                 nc.tensor.matmul_mx(
                     out=dst[:, (e - e0) * C:(e - e0 + 1) * C],
@@ -234,34 +227,38 @@ def tile_moe_ecr_glu_relu_kernel(
                     rhs=quantised[e][0].bitcast(FP8X4), rhs_scale=quantised[e][1],
                     start=True, stop=True,
                 )
-            nc.scalar.copy(y[:, e0 * C:e1 * C], dst[:, 0:(e1 - e0) * C])
+            copy(y[:, e0 * C:e1 * C], dst[:, 0:(e1 - e0) * C])
 
         def gate_branch(e, dst):
             for s in range(PASSES):
                 gate_pass(e, s, dst)
 
-        def value_branch(e, dst):
-            for s in range(PASSES):
-                value_pass(e, s, dst)
+        def value_branch(e, *banks):
+            hidden[e] = keep.tile([P, 2, P, 2], BF16, name="h%d" % e, align_bytes=ALIGN)
+            for (p0, p1), b in zip(halves(e), banks):
+                dst = bank(b)
+                for s in range(PASSES):
+                    first_layer(dst, e, s, w3_t[e], plane_of(w3_planes, W3_RUNS, e), 4 * p0, 4 * p1)
+                nc.vector.tensor_tensor(hidden[e][:, :, p0:p1], by_pair(dst[:, 0:4 * (p1 - p0)]), relu_a[e][:, :, p0:p1], ALU.mult)
 
         gate_branch(0, bank(0))
         gate_branch(1, bank(1))
-        value_branch(0, bank(2))
-        value_branch(1, bank(3))
+        value_branch(0, 2)
+        value_branch(1, 3)
         gather_late_words(4, 4)
         gate_branch(2, bank(6))
-        value_branch(2, bank(5))
-        turn_and_quantise(0, 2, 6)
-        for e, a_bank, b_bank in ((3, 7, 2), (4, 0, 3), (5, 1, 4)):
+        value_branch(2, 5)
+        turn_and_quantise(0, 2, 0, nc.scalar.copy)
+        for e, a_bank, b_banks in ((3, 7, (2,)), (4, 6, (3,)), (5, 1, (4, 5))):
             gate_branch(e, bank(a_bank))
-            value_branch(e, bank(b_bank))
-        turn_and_quantise(2, 3, 3)
-        turn_and_quantise(3, 4, 1)
-        turn_and_quantise(4, 5, 0)
-        turn_and_quantise(5, 6, 2)
-        second_layer(0, 3, bank(4))
-        second_layer(3, 5, bank(6))
-        second_layer(5, 6, bank(7))
+            value_branch(e, *b_banks)
+        turn_and_quantise(2, 3, 3, nc.vector.tensor_copy)
+        turn_and_quantise(3, 4, 1, nc.scalar.copy)
+        turn_and_quantise(4, 5, 6, nc.scalar.copy)
+        turn_and_quantise(5, 6, 2, nc.scalar.copy)
+        second_layer(0, 3, bank(4), nc.vector.tensor_copy)
+        second_layer(3, 5, bank(0), nc.scalar.copy)
+        second_layer(5, 6, bank(7), nc.scalar.copy)
 
         product = [keep.tile([P, T], F32, name="product%d" % r, align_bytes=ALIGN) for r in range(TOP)]
         result = keep.tile([P, T], F32, name="result", align_bytes=ALIGN)

@@ -83,11 +83,11 @@ def tile_moe_ecr_glu_relu_kernel(
         nc.gpsimd.memset(x_live, 0)
         make_identity(nc, ident[:])
 
-        offs_t = keep.tile([P, S // PER_COL], U16, name="offs_t")
+        offs_t = keep.tile([P, S // PER_COL], U16, name="offs_t", align_bytes=ALIGN)
         x_t = [keep.tile([P, T], I32, name="x_t%d" % s, align_bytes=ALIGN) for s in range(PASSES)]
         w1_t, w3_t = {}, {}
         w2_t = keep.tile([P, E * 2 * N], U8, name="w2_t", align_bytes=ALIGN)
-        pos_t = [keep.tile([P, T // PER_COL], U16, name="pos_t%d" % r) for r in range(TOP)]
+        pos_t = [keep.tile([P, T // PER_COL], U16, name="pos_t%d" % r, align_bytes=ALIGN) for r in range(TOP)]
         token_parts = ((0, TURNED_TOKENS), (TURNED_TOKENS, T))
         gate_t = {t0: keep.tile([P, TOP * (t1 - t0)], F32, name="gate_t%d" % t0, align_bytes=ALIGN) for t0, t1 in token_parts}
 
@@ -252,8 +252,8 @@ def tile_moe_ecr_glu_relu_kernel(
         for e, a_bank, b_banks in ((3, 7, (2,)), (4, 6, (3,)), (5, 1, (4, 5))):
             gate_branch(e, bank(a_bank))
             value_branch(e, *b_banks)
-        turn_and_quantise(2, 3, 3, nc.vector.tensor_copy)
-        turn_and_quantise(3, 4, 1, nc.scalar.copy)
+        turn_and_quantise(3, 4, 3, nc.scalar.copy)
+        turn_and_quantise(2, 3, 1, nc.vector.tensor_copy)
         turn_and_quantise(4, 5, 6, nc.scalar.copy)
         turn_and_quantise(5, 6, 2, nc.scalar.copy)
         second_layer(0, 3, bank(4), nc.vector.tensor_copy)

from contextlib import ExitStack

import concourse.mybir as mybir
from concourse.masks import make_identity

K, T, E, C, H, N = 1024, 640, 6, 128, 512, 128
TOP = 4
PAD = 64
S = E * C
P = 128
PASSES = K // 512
PER_COL = 16
FLOPS = 2 * S * (2 * K * H + H * N)
BYTES = PASSES * T * (4 * P + 16) + E * (2 * PASSES * H + N) * (2 * P + 16) + 4 * TOP * T + 2 * P * (S + TOP * T) // PER_COL + 4 * N * T

W1_RUNS = ((0, 3), (3, 6))
W3_RUNS = ((0, 3), (3, 6))
PASS_PITCH = 1536
WORD_TILE = 1024
TURNED_TOKENS = 384

ALIGN = 256

F32 = mybir.dt.float32
BF16 = mybir.dt.bfloat16
I32 = mybir.dt.int32
U32 = mybir.dt.uint32
U16 = mybir.dt.uint16
U8 = mybir.dt.uint8
FP8X4 = mybir.dt.float8_e4m3fn_x4
FP4X4 = mybir.dt.float4_e2m1fn_x4
ACT = mybir.ActivationFunctionType
ALU = mybir.AluOpType


def load_plane(queue, plane, rows):
    by_row = rows.rearrange("g (q r) w -> r q g w", r=4)
    for r in range(4):
        queue.dma_start(
            out=plane[r:P:32, :].bitcast(I32).rearrange("q (g w) -> q g w", g=rows.shape[0]),
            in_=by_row[r].bitcast(I32),
        )


def load_words(nc, tile, words):
    nc.sync.dma_start(
        out=tile[:].bitcast(I32).rearrange("p (g w) -> p g w", g=words.shape[0]),
        in_=words.rearrange("g p b -> p g b").bitcast(I32),
    )


def entries(list_tile, first, last):
    return list_tile[:, first // PER_COL:last // PER_COL]


def by_pair(ap):
    return ap.rearrange("c (p u v) -> c u p v", u=2, v=2)


def tile_moe_ecr_glu_relu_kernel(
    tc, x_words, x_scales, w1_words, w1_scales, w3_words, w3_scales, w2_words, w2_scales,
    gate, offs, pos1, pos2, pos3, pos4, out,
):
    nc = tc.nc
    with ExitStack() as ctx:
        keep = ctx.enter_context(tc.tile_pool(name="keep", bufs=1))
        psum = ctx.enter_context(tc.psum_pool(name="psum", bufs=1))

        def bank(b):
            return psum.tile([P, 512], F32, name="bank", tag="bank%d" % b)

        shared = ctx.enter_context(tc.tile_pool(name="shared", bufs=1))
        x_plane = shared.tile([P, PASSES * PASS_PITCH], U8, name="x_plane", align_bytes=ALIGN, offset=WORD_TILE // 2)
        x_live = x_plane[:].bitcast(I32).rearrange("p (s w) -> p s w", s=PASSES)[:, :, 0:T // 4]
        expert_bytes = PASSES * H
        w1_planes = [keep.tile([P, (e1 - e0) * expert_bytes], U8, name="w1_plane%d" % e0, align_bytes=ALIGN)
                     for e0, e1 in W1_RUNS]
        w3_planes = [keep.tile([P, (e1 - e0) * expert_bytes], U8, name="w3_plane%d" % e0, align_bytes=ALIGN)
                     for e0, e1 in W3_RUNS]
        w2_plane = keep.tile([P, E * N], U8, name="w2_plane", align_bytes=ALIGN)
        y = keep.tile([P, S + PAD], F32, name="y", align_bytes=ALIGN)
        ident = keep.tile([P, P], F32, name="ident", align_bytes=ALIGN)
        nc.gpsimd.memset(x_live, 0)
        make_identity(nc, ident[:])

        offs_t = keep.tile([P, S // PER_COL], U16, name="offs_t", align_bytes=ALIGN)
        x_t = [keep.tile([P, T], I32, name="x_t%d" % s, align_bytes=ALIGN) for s in range(PASSES)]
        w1_t, w3_t = {}, {}
        w2_t = keep.tile([P, E * 2 * N], U8, name="w2_t", align_bytes=ALIGN)
        pos_t = [keep.tile([P, T // PER_COL], U16, name="pos_t%d" % r, align_bytes=ALIGN) for r in range(TOP)]
        token_parts = ((0, TURNED_TOKENS), (TURNED_TOKENS, T))
        gate_t = {t0: keep.tile([P, TOP * (t1 - t0)], F32, name="gate_t%d" % t0, align_bytes=ALIGN) for t0, t1 in token_parts}

        def load_tokens(s):
            nc.sync.dma_start(out=x_t[s][:], in_=x_words[s].rearrange("p t r -> p (t r)").bitcast(I32))

        def load_rows(planes, scales, runs, run):
            e0, e1 = runs[run]
            load_plane(nc.sync, planes[run][:], scales[e0:e1].rearrange("e s q w -> (e s) q w"))

        def load_experts(found, words, name, e0, e1):
            tile = keep.tile([P, (e1 - e0) * 2 * expert_bytes], U8, name="%s_t%d" % (name, e0), align_bytes=ALIGN)
            load_words(nc, tile, words[e0:e1].rearrange("e s p b -> (e s) p b"))
            for e in range(e0, e1):
                found[e] = tile[:, (e - e0) * 2 * expert_bytes:(e - e0 + 1) * 2 * expert_bytes]

        def load_w1(e0, e1):
            load_experts(w1_t, w1_words, "w1", e0, e1)

        def load_w3(e0, e1):
            load_experts(w3_t, w3_words, "w3", e0, e1)

        load_tokens(0)
        nc.sync.dma_start(offs_t[:], offs)
        load_tokens(1)
        x_rows = x_scales.rearrange("s (q r) t -> r q s t", r=4)
        for r in range(4):
            nc.sync.dma_start(out=x_live[r:P:32], in_=x_rows[r].bitcast(I32))
        load_w1(0, 2)
        load_rows(w1_planes, w1_scales, W1_RUNS, 0)
        load_rows(w3_planes, w3_scales, W3_RUNS, 0)
        load_w3(0, 2)
        load_w1(2, 3)
        load_w3(2, 3)
        load_w1(3, 4)
        load_rows(w1_planes, w1_scales, W1_RUNS, 1)
        load_rows(w3_planes, w3_scales, W3_RUNS, 1)
        load_w3(3, 4)
        for e in range(4, E):
            load_w1(e, e + 1)
            load_w3(e, e + 1)
        load_plane(nc.sync, w2_plane[:], w2_scales.rearrange("e s q w -> (e s) q w"))
        load_words(nc, w2_t, w2_words.rearrange("e s p b -> (e s) p b"))

        def load_gate(part, r0, r1):
            t0, t1 = token_parts[part]
            nc.sync.dma_start(out=gate_t[t0][:].rearrange("n (r t) -> n r t", r=TOP)[:, r0:r1, :],
                              in_=gate[r0:r1, :, t0:t1].rearrange("r n t -> n r t"))

        for r0, lists in ((0, (pos1, pos2)), (2, (pos3, pos4))):
            load_gate(0, r0, r0 + 2)
            for j, pos in enumerate(lists):
                nc.sync.dma_start(pos_t[r0 + j][:], pos)
        load_gate(1, 0, TOP)

        nc.scalar.activation(y[:, S:S + PAD], ident[:, 0:PAD], ACT.Relu, scale=-1.0)

        slot_words, slot_planes = {}, {}

        def gather(found, e0, s, window, dst):
            nc.vector.tensor_copy(dst[:], window.indirect(entries(offs_t, e0 * C, (e0 + 2) * C)))
            for j in range(2):
                found[e0 + j, s] = dst[:, j * C:(j + 1) * C]

        for s in range(PASSES):
            dst = keep.tile([P, 2 * C], U32, name="words0%d" % s, align_bytes=ALIGN)
            gather(slot_words, 0, s, x_t[s][:].bitcast(U32), dst)
        for e0 in (0, 2, 4):
            for s in range(PASSES):
                dst = keep.tile([P, 2 * C], U8, name="bytes%d%d" % (e0, s), align_bytes=ALIGN)
                gather(slot_planes, e0, s, x_plane[:, s * PASS_PITCH:s * PASS_PITCH + T], dst)

        def gather_late_words(e0, first_tile):
            for s in range(PASSES):
                dst = shared.tile([P, 2 * C], U32, name="words%d%d" % (e0, s), align_bytes=ALIGN,
                                  offset=(first_tile + s) * WORD_TILE)
                gather(slot_words, e0, s, x_t[s][:].bitcast(U32), dst)

        gather_late_words(2, 0)

        def first_layer(dst, e, s, words, plane, i0=0, i1=H):
            nc.tensor.matmul_mx(
                out=dst[:, 0:i1 - i0],
                lhsT=slot_words[e, s].bitcast(FP8X4), lhsT_scale=slot_planes[e, s],
                rhs=words[:, 2 * (s * H + i0):2 * (s * H + i1)].bitcast(FP4X4),
                rhs_scale=plane[:, s * H + i0:s * H + i1],
                start=(s == 0), stop=(s == PASSES - 1),
            )

        hidden, quantised = {}, {}

        relu_a = {}

        def plane_of(planes, runs, e):
            run = 0 if e < runs[0][1] else 1
            j = e - runs[run][0]
            return planes[run][:, j * expert_bytes:(j + 1) * expert_bytes]

        def halves(e):
            return ((0, P),) if e < E - 1 else ((0, P // 2), (P // 2, P))

        def gate_pass(e, s, dst):
            first_layer(dst, e, s, w1_t[e], plane_of(w1_planes, W1_RUNS, e))
            if s == PASSES - 1:
                if e == 1:
                    relu_a[e] = shared.tile([P, 2, P, 2], F32, name="relu_a1", align_bytes=ALIGN, offset=4 * WORD_TILE)
                else:
                    relu_a[e] = keep.tile([P, 2, P, 2], F32, name="relu_a%d" % e, align_bytes=ALIGN)
                for p0, p1 in halves(e):
                    nc.scalar.activation(relu_a[e][:, :, p0:p1], by_pair(dst[:])[:, :, p0:p1], ACT.Relu)

        def turn_and_quantise(e0, e1, room_bank, copy):
            n = e1 - e0
            room = bank(room_bank)[:, 0:n * 2 * P]
            for e in range(e0, e1):
                pairs = hidden[e][:].rearrange("c u p v -> c (u p v)").bitcast(F32)
                for u in range(2):
                    col = ((e - e0) * 2 + u) * P
                    nc.tensor.transpose(room[:, col:col + P], pairs[:, u * P:(u + 1) * P], ident[:])
            turned = keep.tile([P, n, C, 2], F32, name="turned%d" % e0, align_bytes=ALIGN)
            copy(turned[:], room.rearrange("p (e u c) -> p e c u", e=n, u=2))
            h_words = keep.tile([P, n * C], U32, name="h_words%d" % e0, align_bytes=ALIGN)
            h_plane = keep.tile([P, n * C], U8, name="h_plane%d" % e0, align_bytes=ALIGN)
            nc.vector.quantize_mx(
                out=h_words[:].bitcast(FP8X4), scales=h_plane[:],
                in_=turned[:].rearrange("p e c u -> p (e c u)").bitcast(BF16),
            )
            for j in range(n):
                quantised[e0 + j] = (h_words[:, j * C:(j + 1) * C], h_plane[:, j * C:(j + 1) * C])

        def second_layer(e0, e1, dst, copy):
            for e in range(e0, e1):
                nc.tensor.matmul_mx(
                    out=dst[:, (e - e0) * C:(e - e0 + 1) * C],
                    lhsT=w2_t[:, e * 2 * N:(e + 1) * 2 * N].bitcast(FP4X4),
                    lhsT_scale=w2_plane[:, e * N:(e + 1) * N],
                    rhs=quantised[e][0].bitcast(FP8X4), rhs_scale=quantised[e][1],
                    start=True, stop=True,
                )
            copy(y[:, e0 * C:e1 * C], dst[:, 0:(e1 - e0) * C])

        def gate_branch(e, dst):
            for s in range(PASSES):
                gate_pass(e, s, dst)

        def value_branch(e, *banks):
            hidden[e] = keep.tile([P, 2, P, 2], BF16, name="h%d" % e, align_bytes=ALIGN)
            for (p0, p1), b in zip(halves(e), banks):
                dst = bank(b)
                for s in range(PASSES):
                    first_layer(dst, e, s, w3_t[e], plane_of(w3_planes, W3_RUNS, e), 4 * p0, 4 * p1)
                nc.vector.tensor_tensor(hidden[e][:, :, p0:p1], by_pair(dst[:, 0:4 * (p1 - p0)]), relu_a[e][:, :, p0:p1], ALU.mult)

        gate_branch(0, bank(0))
        gate_branch(1, bank(1))
        value_branch(0, 2)
        value_branch(1, 3)
        gather_late_words(4, 4)
        gate_branch(2, bank(6))
        value_branch(2, 5)
        turn_and_quantise(0, 2, 0, nc.scalar.copy)
        for e, a_bank, b_banks in ((3, 7, (2,)), (4, 6, (3,)), (5, 1, (4, 5))):
            gate_branch(e, bank(a_bank))
            value_branch(e, *b_banks)
        turn_and_quantise(3, 4, 3, nc.scalar.copy)
        turn_and_quantise(2, 3, 1, nc.vector.tensor_copy)
        turn_and_quantise(4, 5, 6, nc.scalar.copy)
        turn_and_quantise(5, 6, 2, nc.scalar.copy)
        second_layer(0, 3, bank(4), nc.vector.tensor_copy)
        second_layer(3, 5, bank(0), nc.scalar.copy)
        second_layer(5, 6, bank(7), nc.scalar.copy)

        product = [keep.tile([P, T], F32, name="product%d" % r, align_bytes=ALIGN) for r in range(TOP)]
        result = keep.tile([P, T], F32, name="result", align_bytes=ALIGN)

        def fetch(r, t0, t1):
            nc.vector.tensor_tensor(product[r][:, t0:t1], y[:].indirect(entries(pos_t[r], t0, t1)),
                                    gate_t[t0][:, r * (t1 - t0):(r + 1) * (t1 - t0)], ALU.mult)

        chunks = TURNED_TOKENS // P
        sums = [bank(c) for c in range(chunks)]
        for r in range(TOP):
            fetch(r, 0, TURNED_TOKENS)
            for c in range(chunks):
                nc.tensor.matmul(sums[c][:, 0:P], lhsT=product[r][:, c * P:(c + 1) * P], rhs=ident[:],
                                 is_transpose=True, start=(r == 0), stop=(r == TOP - 1))
        back = bank(chunks)
        for c in range(chunks):
            by_token = keep.tile([P, P], F32, name="by_token%d" % c, align_bytes=ALIGN)
            nc.scalar.copy(by_token[:], sums[c][:, 0:P])
            nc.tensor.transpose(back[:, c * P:(c + 1) * P], by_token[:], ident[:])
        nc.scalar.copy(result[:, 0:TURNED_TOKENS], back[:, 0:TURNED_TOKENS])
        nc.scalar.dma_start(out=out[:, 0:TURNED_TOKENS], in_=result[:, 0:TURNED_TOKENS])

        rest = slice(TURNED_TOKENS, T)
        partial = [keep.tile([P, T], F32, name="partial%d" % j, align_bytes=ALIGN) for j in range(TOP - 2)]
        for r in range(TOP - 1):
            fetch(r, TURNED_TOKENS, T)
        nc.vector.tensor_tensor(partial[0][:, rest], product[0][:, rest], product[1][:, rest], ALU.add)
        fetch(TOP - 1, TURNED_TOKENS, T)
        last_chunks = [slice(t0, t0 + P) for t0 in range(TURNED_TOKENS, T, P)]
        for ts in last_chunks:
            nc.vector.tensor_tensor(partial[1][:, ts], partial[0][:, ts], product[2][:, ts], ALU.add)
        for ts, queue in zip(last_chunks, (nc.scalar, nc.sync)):
            nc.vector.tensor_tensor(result[:, ts], partial[1][:, ts], product[3][:, ts], ALU.add)
            queue.dma_start(out=out[:, ts], in_=result[:, ts])
